import numpy as np
import ml_dtypes


def mxq(x, axis, fmt="e4m3"):
    dtype, down = {"e4m3": (ml_dtypes.float8_e4m3fn, 7), "e5m2": (ml_dtypes.float8_e5m2, 14)}[fmt]
    v = np.moveaxis(np.asarray(x, np.float32).astype(ml_dtypes.bfloat16).astype(np.float64), axis, -1)
    blocks = v.reshape(v.shape[:-1] + (-1, 32))
    amax = np.abs(blocks).max(-1, keepdims=True)
    byte = np.maximum(np.where(amax > 0, np.frexp(amax)[1] - 1 + 127, 0) - down, 1)
    scale = np.exp2(byte - 127.0)
    codes = (blocks / scale).astype(np.float32).astype(dtype).astype(np.float64)
    return np.moveaxis((codes * scale).reshape(v.shape), -1, axis)


WIDE = False


def mx_kscale(k):
    if not WIDE:
        return np.ones(k)
    levels = np.array([10, -10, 5, -5, 0])
    if k % 512:
        return np.exp2(np.random.permutation(np.resize(levels, k // 32))).repeat(32)
    a = np.empty((k // 512, 16))
    for p in range(k // 512):
        a[p, :8] = np.random.permutation(np.resize(levels, 8))
        for g in range(8):
            far = levels[np.abs(levels - a[p, g]) >= 10]
            a[p, g + 8] = far[np.random.randint(len(far))]
    return np.exp2(a.ravel()).repeat(32)


def f64(x):
    return np.asarray(x).astype(np.float64)


def striped(idx):
    return np.tile(idx.reshape(-1, 16).T, (8, 1)).astype(np.uint16)


def unstriped(offs):
    return offs[:16].T.reshape(-1).astype(np.int64)


E2M1 = np.array([0.0, 0.5, 1.0, 1.5, 2.0, 3.0, 4.0, 6.0, -0.0, -0.5, -1.0, -1.5, -2.0, -3.0, -4.0, -6.0])


def pack_weight(w, fmt):
    k, n = w.shape
    w = f64(np.asarray(w, np.float32).astype(ml_dtypes.bfloat16)).reshape(k // 32, 32, n)
    amax = np.abs(w).max(1)
    if fmt == "e4m3":
        byte = np.frexp(amax)[1] - 1 + 127 - 7
    else:
        mant, ex = np.frexp(amax / 6.0)
        byte = np.where(mant > 0.5, ex, ex - 1) + 127
    byte = np.clip(np.where(amax > 0, byte, 1), 1, 254)
    scaled = (w * np.exp2(127.0 - byte)[:, None, :]).reshape(k, n).astype(np.float32)
    by_word = np.ascontiguousarray(scaled.reshape(k // 512, 128, 4, n).transpose(0, 1, 3, 2))
    if fmt == "e4m3":
        words = by_word.astype(ml_dtypes.float8_e4m3fn).view(np.uint8)
    else:
        c = by_word.astype(ml_dtypes.float4_e2m1fn).view(np.uint8) & 0xF
        words = (c[..., 0::2] | (c[..., 1::2] << 4)).reshape(k // 512, 128, 2 * n)
    return np.ascontiguousarray(words), np.ascontiguousarray(byte.astype(np.uint8).reshape(k // 512, 16, n))


def unpack_weight(words, scales, fmt):
    g, _, n = scales.shape
    words = np.ascontiguousarray(words).reshape(g, 128, n, -1)
    if fmt == "e4m3":
        vals = words.view(ml_dtypes.float8_e4m3fn).astype(np.float64)
    else:
        nib = np.empty((g, 128, n, 4), np.uint8)
        nib[..., 0::2] = words & 0xF
        nib[..., 1::2] = words >> 4
        vals = E2M1[nib]
    vals = vals * np.repeat(np.exp2(scales.astype(np.float64) - 127.0), 8, axis=1)[..., None]
    return vals.transpose(0, 1, 3, 2).reshape(g * 512, n)


def gelu(v):
    return 0.5 * v * (1.0 + np.tanh(np.sqrt(2.0 / np.pi) * (v + 0.044715 * v**3)))


def bf(x):
    return np.asarray(x, np.float32).astype(ml_dtypes.bfloat16)

def planes(Y):
    n, m = Y.shape
    b = f64(bf(Y)).reshape(n // 32, 32, m)
    amax = np.abs(b).max(1)
    byte = np.clip(np.where(amax > 0, np.frexp(amax)[1] - 1 + 127 - 7, 1), 1, 254)
    codes = (b * np.exp2(127.0 - byte)[:, None, :]).reshape(n, m).astype(np.float32).astype(ml_dtypes.float8_e4m3fn).view(np.uint8)
    words = codes.reshape(n // 512, 128, 4, m).transpose(0, 1, 3, 2)
    return np.ascontiguousarray(words), np.ascontiguousarray(byte.astype(np.uint8).reshape(n // 512, 16, m))


K, T, S, H, N = 1024, 4096, 1024, 512, 1024

def setup_inputs():
    n = np.random.standard_normal
    s = mx_kscale(K)[:, None]
    u = mx_kscale(H)[:, None]
    tab_words, tab_scales = pack_weight(n((K, T)) * s, "e4m3")
    offs = striped(np.random.permutation(T)[:S])
    wl = (0.7 * n((K, H)) / np.sqrt(K) / s).astype(np.float32)
    wr_words, wr_scales = pack_weight(0.7 * n((K, H)) / np.sqrt(K) / s, "e2m1")
    mob = (np.exp(0.3 * n(H)) * u[:, 0]).astype(np.float32)
    wo_words, wo_scales = pack_weight(2.0 * n((H, N)) / np.sqrt(H) * np.exp(0.8 * n(N)) / u, "e4m3")
    return {"tab_words": tab_words, "tab_scales": tab_scales, "offs": offs,
            "wl": wl, "wr_words": wr_words, "wr_scales": wr_scales,
            "mob": mob, "wo_words": wo_words, "wo_scales": wo_scales}

def reference(tab_words, tab_scales, offs, wl, wr_words, wr_scales, mob, wo_words, wo_scales):
    v = unpack_weight(tab_words, tab_scales, "e4m3")[:, unstriped(offs)]
    wr = unpack_weight(wr_words, wr_scales, "e2m1")
    wo = unpack_weight(wo_words, wo_scales, "e4m3")
    rl = np.exp(mxq(f64(wl), 0, "e4m3").T @ v)
    rr = np.exp(wr.T @ v)
    h = f64(mob)[:, None] * (1.0 / (rl + rr))
    y = wo.T @ mxq(h, 0, "e4m3")
    words, scales = planes(y)
    return y, words, scales

@@ -1,0 +1,264 @@
+from contextlib import ExitStack
+
+import concourse.mybir as mybir
+
+K, T, S, H, N = 1024, 4096, 1024, 512, 1024
+FLOPS = 2 * K * H * S * 2 + 2 * H * N * S
+
+F32 = mybir.dt.float32
+BF16 = mybir.dt.bfloat16
+I32 = mybir.dt.int32
+U32 = mybir.dt.uint32
+U16 = mybir.dt.uint16
+U8 = mybir.dt.uint8
+FP8X4 = mybir.dt.float8_e4m3fn_x4
+FP4X4 = mybir.dt.float4_e2m1fn_x4
+ACT = mybir.ActivationFunctionType
+ALU = mybir.AluOpType
+
+P = 128
+PACK = 4
+KP = P * PACK
+PASSES = K // KP
+GROUPS = N // KP
+CHUNK = 512
+CHUNKS = S // CHUNK
+PIECES = [128, 256, 256, 256, 128]
+WORD_STORES = [1, 3, 4]
+BANKS = 8
+
+
+def tile_list_face_transmissibility_kernel(
+    tc, tab_words, tab_scales, offs, wl, wr_words, wr_scales, mob, wo_words, wo_scales, out_0, out_1, out_2
+):
+    nc = tc.nc
+    with ExitStack() as ctx:
+        keep = ctx.enter_context(tc.tile_pool(name="keep", bufs=1))
+        psum = ctx.enter_context(tc.psum_pool(name="psum", bufs=1))
+
+        def sb(shape, dtype, name):
+            return keep.tile(shape, dtype, name=name, align_bytes=64)
+
+        def bank(b):
+            return psum.tile([P, 512], F32, name="bank%d" % (b % BANKS))
+
+        offsets = keep.tile([P, S // 16], U16, name="offsets")
+        nc.sync.dma_start(offsets[:], offs)
+
+        tab_sc = sb([P, T], U8, "tab_sc")
+        nc.vector.memset(tab_sc[:].bitcast(I32), 0)
+        v_sc1 = sb([P, S], U8, "v_sc1")
+        nc.vector.memset(v_sc1[:].bitcast(I32), 0)
+        wr_sc_raw = sb([P, PASSES * H], U8, "wr_sc_raw")
+        nc.gpsimd.memset(wr_sc_raw[:].bitcast(I32), 0)
+        wo_sc_raw = sb([P, N], U8, "wo_sc_raw")
+        nc.gpsimd.memset(wo_sc_raw[:].bitcast(I32), 0)
+
+        warm = sb([P, 1], F32, "warm")
+        nc.gpsimd.memset(warm[:], 0.0)
+        warm_out = sb([P, 1], F32, "warm_out")
+        nc.scalar.activation(warm_out[:], warm[:], ACT.Exp)
+
+        wr_raw = sb([P, PASSES * 2 * H], U8, "wr_raw")
+        nc.sync.dma_start(
+            wr_raw[:].bitcast(I32).rearrange("p (a n) -> p a n", a=PASSES),
+            wr_words.bitcast(I32).rearrange("a p n -> p a n"),
+        )
+        mob_sb = sb([P, PACK], F32, "mob_sb")
+        nc.sync.dma_start(mob_sb[:], mob.rearrange("(p t) -> p t", t=PACK))
+        tab_sc_rows = tab_scales.rearrange("a (q r) n -> r q a n", r=4)
+        for r in range(4):
+            nc.sync.dma_start(tab_sc[r:P:16, :].bitcast(I32), tab_sc_rows[r].bitcast(I32))
+        tab_w = [sb([P, T], I32, "tab_w%d" % a) for a in range(PASSES)]
+
+        def load_table(a):
+            nc.sync.dma_start(tab_w[a][:], tab_words[a].rearrange("p n t -> p (n t)").bitcast(I32))
+
+        load_table(0)
+        for q in range(4):
+            nc.sync.dma_start(
+                wr_sc_raw[32 * q : 32 * q + 4, :].bitcast(I32).rearrange("r (a n) -> r a n", a=PASSES),
+                wr_scales[:, 4 * q : 4 * q + 4, :].bitcast(I32).rearrange("a r n -> r a n"),
+            )
+        v_sc0 = sb([P, S], U8, "v_sc0")
+        nc.vector.tensor_copy(v_sc0[:], tab_sc[:].indirect(offsets[:]))
+        nc.sync.dma_start(v_sc1[0:112, :].bitcast(I32), v_sc0[16:P, :].bitcast(I32))
+        v_sc = [v_sc0, v_sc1]
+        load_table(1)
+        wl_parts = [(0, 0, H), (1, 0, H // 2), (1, H // 2, H // 2)]
+        wl_raw = []
+        for a, c0, w in wl_parts:
+            t_ = sb([P, PACK, w], F32, "wl_raw%d_%d" % (a, c0))
+            nc.sync.dma_start(
+                t_[:], wl[a * KP : (a + 1) * KP, c0 : c0 + w].rearrange("(p j) c -> p j c", j=PACK)
+            )
+            wl_raw.append(t_)
+        wo_raw = sb([P, N], I32, "wo_raw")
+        nc.sync.dma_start(wo_raw[:], wo_words[0].rearrange("p n t -> p (n t)").bitcast(I32))
+        for q in range(4):
+            nc.sync.dma_start(
+                wo_sc_raw[32 * q : 32 * q + 4, :].bitcast(I32),
+                wo_scales[0, 4 * q : 4 * q + 4, :].bitcast(I32),
+            )
+
+        wr_w = sb([P, PASSES * 2 * H], U8, "wr_w")
+        nc.vector.tensor_copy(
+            wr_w[:].rearrange("p (a t m b) -> p a m t b", a=PASSES, t=PACK, b=2),
+            wr_raw[:].rearrange("p (a m t b) -> p a m t b", a=PASSES, t=PACK, b=2),
+        )
+        wr_sc = sb([P, PASSES * H], U8, "wr_sc")
+        nc.vector.tensor_copy(
+            wr_sc[:].rearrange("p (a t m) -> p a m t", a=PASSES, t=PACK),
+            wr_sc_raw[:].rearrange("p (a m t) -> p a m t", a=PASSES, t=PACK),
+        )
+        inv_mob = sb([P, PACK], F32, "inv_mob")
+        nc.vector.reciprocal(inv_mob[:], mob_sb[:])
+
+        v_w = {}
+        for a in range(PASSES):
+            for c in range(CHUNKS):
+                t_ = sb([P, CHUNK], U32, "v_w%d_%d" % (a, c))
+                cols = CHUNK // 16
+                nc.vector.tensor_copy(
+                    t_[:], tab_w[a][:].bitcast(U32).indirect(offsets[:, c * cols : (c + 1) * cols])
+                )
+                v_w[a, c] = t_
+
+        def first_stage(lhs, lhs_scale, name, order):
+            acc = {}
+            for a, c in order:
+                if True:
+                    for t in range(PACK):
+                        if a == 0:
+                            acc[c, t] = bank(c * PACK + t)
+                        nc.tensor.matmul_mx(
+                            acc[c, t][:],
+                            lhsT=lhs(a, t),
+                            lhsT_scale=lhs_scale(a, t),
+                            rhs=v_w[a, c][:].bitcast(FP8X4),
+                            rhs_scale=v_sc[a][:, c * CHUNK : (c + 1) * CHUNK],
+                            start=(a == 0),
+                            stop=(a == PASSES - 1),
+                        )
+            res = {}
+            for c in range(CHUNKS):
+                for t in range(PACK):
+                    res[c, t] = sb([P, CHUNK], F32, "%s%d_%d" % (name, c, t))
+                    nc.scalar.activation(res[c, t][:], acc[c, t][:], ACT.Exp)
+            return res
+
+        rr = first_stage(
+            lambda a, t: wr_w[:, (a * PACK + t) * 2 * P : (a * PACK + t + 1) * 2 * P].bitcast(FP4X4),
+            lambda a, t: wr_sc[:, (a * PACK + t) * P : (a * PACK + t + 1) * P],
+            "rr",
+            [(a, c) for a in range(PASSES) for c in range(CHUNKS)],
+        )
+
+        wl_bf = [sb([P, PACK * H], BF16, "wl_bf%d" % a) for a in range(PASSES)]
+        wl_w = [sb([P, H], U32, "wl_w%d" % a) for a in range(PASSES)]
+        wl_sc = [sb([P, H], U8, "wl_sc%d" % a) for a in range(PASSES)]
+        for (a, c0, w), raw in zip(wl_parts, wl_raw):
+            nc.vector.tensor_copy(
+                wl_bf[a][:].rearrange("p (t m j) -> p m j t", t=PACK, j=PACK)[:, c0 // PACK : (c0 + w) // PACK],
+                raw[:].rearrange("p j (m t) -> p m j t", t=PACK),
+            )
+            if c0 + w == H:
+                nc.vector.quantize_mx(wl_w[a][:].bitcast(FP8X4), wl_sc[a][:], wl_bf[a][:])
+
+        rl = first_stage(
+            lambda a, t: wl_w[a][:, t * P : (t + 1) * P].bitcast(FP8X4),
+            lambda a, t: wl_sc[a][:, t * P : (t + 1) * P],
+            "rl",
+            [(a, c) for c in range(CHUNKS) for a in range(PASSES)],
+        )
+
+        total = [sb([P, S], F32, "total%d" % t) for t in range(PACK)]
+        for c in range(CHUNKS):
+            for t in range(PACK):
+                nc.vector.tensor_tensor(
+                    total[t][:, c * CHUNK : (c + 1) * CHUNK], rl[c, t][:], rr[c, t][:], ALU.add
+                )
+
+        wo_w = sb([P, N], I32, "wo_w")
+        nc.vector.tensor_copy(
+            wo_w[:].rearrange("p (g t m) -> p g m t", g=GROUPS, t=PACK),
+            wo_raw[:].rearrange("p (g m t) -> p g m t", g=GROUPS, t=PACK),
+        )
+        wo_sc = sb([P, N], U8, "wo_sc")
+        nc.vector.tensor_copy(
+            wo_sc[:].rearrange("p (g t m) -> p g m t", g=GROUPS, t=PACK),
+            wo_sc_raw[:].rearrange("p (g m t) -> p g m t", g=GROUPS, t=PACK),
+        )
+
+        y_sc = sb([P, GROUPS, S], U8, "y_sc")
+        y_w = sb([P, GROUPS, S], I32, "y_w")
+        out_words = out_1.rearrange("g p n t -> p g (n t)").bitcast(I32)
+        starts = [sum(PIECES[:i]) for i in range(len(PIECES) + 1)]
+        h_w, h_sc = {}, {}
+        used = []
+
+        def make_h(i):
+            j0, w = starts[i], PIECES[i]
+            root = sb([P, PACK, w], F32, "root%d" % i)
+            for t in range(PACK):
+                nc.scalar.activation(
+                    root[:, t, :],
+                    total[t][:, j0 : j0 + w],
+                    ACT.Abs_reciprocal_sqrt,
+                    scale=inv_mob[:, t : t + 1],
+                )
+            h_bf = sb([P, w * PACK], BF16, "h_bf%d" % i)
+            by_line = root[:].rearrange("p t (c i) -> p c t i", i=4)
+            nc.vector.tensor_tensor(
+                h_bf[:].rearrange("p (c i t) -> p c t i", i=4, t=PACK), by_line, by_line, ALU.mult
+            )
+            h_w[i] = sb([P, w], U32, "h_w%d" % i)
+            h_sc[i] = sb([P, w], U8, "h_sc%d" % i)
+            nc.vector.quantize_mx(h_w[i][:].bitcast(FP8X4), h_sc[i][:], h_bf[:])
+
+        def make_y(i):
+            j0, w = starts[i], PIECES[i]
+            cols = slice(j0, j0 + w)
+            per_bank = 512 // w
+            for g in range(GROUPS):
+                y = sb([P, PACK, w], F32, "y%d_%d" % (i, g))
+                for t0 in range(0, PACK, per_bank):
+                    acc = bank(len(used))
+                    used.append(i)
+                    for e in range(per_bank):
+                        s0 = (g * PACK + t0 + e) * P
+                        nc.tensor.matmul_mx(
+                            acc[:, e * w : (e + 1) * w],
+                            lhsT=wo_w[:, s0 : s0 + P].bitcast(FP8X4),
+                            lhsT_scale=wo_sc[:, s0 : s0 + P],
+                            rhs=h_w[i][:].bitcast(FP8X4),
+                            rhs_scale=h_sc[i][:],
+                            start=True,
+                            stop=True,
+                        )
+                    nc.scalar.copy(y[:, t0 : t0 + per_bank, :].rearrange("p e j -> p (e j)"), acc[:])
+                nc.sync.dma_start(
+                    out_0[g * KP : (g + 1) * KP, cols].rearrange("(p t) j -> p t j", t=PACK), y[:]
+                )
+                y_bf = sb([P, w * PACK], BF16, "y_bf%d_%d" % (i, g))
+                nc.vector.tensor_copy(
+                    y_bf[:].rearrange("p (c i t) -> p c t i", i=4, t=PACK),
+                    y[:].rearrange("p t (c i) -> p c t i", i=4),
+                )
+                nc.vector.quantize_mx(y_w[:, g, cols].bitcast(FP8X4), y_sc[:, g, cols], y_bf[:])
+            if i in WORD_STORES:
+                first = ([-1] + WORD_STORES)[WORD_STORES.index(i)] + 1
+                span = slice(starts[first], j0 + w)
+                nc.sync.dma_start(out_words[:, :, span], y_w[:, :, span])
+
+        make_h(0)
+        for i in range(len(PIECES)):
+            if i + 1 < len(PIECES):
+                make_h(i + 1)
+            make_y(i)
+
+        for q in range(4):
+            nc.sync.dma_start(
+                out_2[:, 4 * q : 4 * q + 4, :].bitcast(I32).rearrange("g r n -> r g n"),
+                y_sc[32 * q : 32 * q + 4, :, :].bitcast(I32),
+            )

@@ -24,7 +24,10 @@ GROUPS = N // KP
 CHUNK = 512
 CHUNKS = S // CHUNK
 PIECES = [128, 256, 256, 256, 128]
-WORD_STORES = [1, 3, 4]
+Y_STORES = [[0], [1], [2], [3, 4]]
+WORD_STORES = [[0, 1], [2, 3, 4]]
+VECTOR_BANKS = (1, 3)
+PLANE_LAG = 2
 BANKS = 8
 
 
@@ -54,38 +57,10 @@ def tile_list_face_transmissibility_kernel(
         wo_sc_raw = sb([P, N], U8, "wo_sc_raw")
         nc.gpsimd.memset(wo_sc_raw[:].bitcast(I32), 0)
 
-        warm = sb([P, 1], F32, "warm")
-        nc.gpsimd.memset(warm[:], 0.0)
-        warm_out = sb([P, 1], F32, "warm_out")
-        nc.scalar.activation(warm_out[:], warm[:], ACT.Exp)
-
-        wr_raw = sb([P, PASSES * 2 * H], U8, "wr_raw")
-        nc.sync.dma_start(
-            wr_raw[:].bitcast(I32).rearrange("p (a n) -> p a n", a=PASSES),
-            wr_words.bitcast(I32).rearrange("a p n -> p a n"),
-        )
-        mob_sb = sb([P, PACK], F32, "mob_sb")
-        nc.sync.dma_start(mob_sb[:], mob.rearrange("(p t) -> p t", t=PACK))
-        tab_sc_rows = tab_scales.rearrange("a (q r) n -> r q a n", r=4)
-        for r in range(4):
-            nc.sync.dma_start(tab_sc[r:P:16, :].bitcast(I32), tab_sc_rows[r].bitcast(I32))
         tab_w = [sb([P, T], I32, "tab_w%d" % a) for a in range(PASSES)]
-
-        def load_table(a):
+        for a in range(PASSES):
             nc.sync.dma_start(tab_w[a][:], tab_words[a].rearrange("p n t -> p (n t)").bitcast(I32))
-
-        load_table(0)
-        for q in range(4):
-            nc.sync.dma_start(
-                wr_sc_raw[32 * q : 32 * q + 4, :].bitcast(I32).rearrange("r (a n) -> r a n", a=PASSES),
-                wr_scales[:, 4 * q : 4 * q + 4, :].bitcast(I32).rearrange("a r n -> r a n"),
-            )
-        v_sc0 = sb([P, S], U8, "v_sc0")
-        nc.vector.tensor_copy(v_sc0[:], tab_sc[:].indirect(offsets[:]))
-        nc.sync.dma_start(v_sc1[0:112, :].bitcast(I32), v_sc0[16:P, :].bitcast(I32))
-        v_sc = [v_sc0, v_sc1]
-        load_table(1)
-        wl_parts = [(0, 0, H), (1, 0, H // 2), (1, H // 2, H // 2)]
+        wl_parts = [(0, 0, H), (1, 0, H)]
         wl_raw = []
         for a, c0, w in wl_parts:
             t_ = sb([P, PACK, w], F32, "wl_raw%d_%d" % (a, c0))
@@ -100,6 +75,30 @@ def tile_list_face_transmissibility_kernel(
                 wo_sc_raw[32 * q : 32 * q + 4, :].bitcast(I32),
                 wo_scales[0, 4 * q : 4 * q + 4, :].bitcast(I32),
             )
+
+        wr_raw = sb([P, PASSES * 2 * H], U8, "wr_raw")
+        nc.scalar.dma_start(
+            wr_raw[:].bitcast(I32).rearrange("p (a n) -> p a n", a=PASSES),
+            wr_words.bitcast(I32).rearrange("a p n -> p a n"),
+        )
+        mob_sb = sb([P, PACK], F32, "mob_sb")
+        nc.scalar.dma_start(mob_sb[:], mob.rearrange("(p t) -> p t", t=PACK))
+        tab_sc_rows = tab_scales.rearrange("a (q r) n -> r q a n", r=4)
+        for r in range(4):
+            nc.scalar.dma_start(tab_sc[r:P:16, :].bitcast(I32), tab_sc_rows[r].bitcast(I32))
+        for q in range(4):
+            nc.scalar.dma_start(
+                wr_sc_raw[32 * q : 32 * q + 4, :].bitcast(I32).rearrange("r (a n) -> r a n", a=PASSES),
+                wr_scales[:, 4 * q : 4 * q + 4, :].bitcast(I32).rearrange("a r n -> r a n"),
+            )
+        v_sc0 = sb([P, S], U8, "v_sc0")
+        nc.vector.tensor_copy(v_sc0[:], tab_sc[:].indirect(offsets[:]))
+        nc.scalar.dma_start(v_sc1[0:112, :].bitcast(I32), v_sc0[16:P, :].bitcast(I32))
+        v_sc = [v_sc0, v_sc1]
+        warm = sb([P, 1], F32, "warm")
+        nc.gpsimd.memset(warm[:], 0.0)
+        warm_out = sb([P, 1], F32, "warm_out")
+        nc.scalar.activation(warm_out[:], warm[:], ACT.Exp)
 
         wr_w = sb([P, PASSES * 2 * H], U8, "wr_w")
         nc.vector.tensor_copy(
@@ -216,15 +215,21 @@ def tile_list_face_transmissibility_kernel(
             h_sc[i] = sb([P, w], U8, "h_sc%d" % i)
             nc.vector.quantize_mx(h_w[i][:].bitcast(FP8X4), h_sc[i][:], h_bf[:])
 
+        y_tiles = {}
+        for group in Y_STORES:
+            width = starts[group[-1] + 1] - starts[group[0]]
+            for g in range(GROUPS):
+                tile_ = sb([P, PACK, width], F32, "y%d_%d" % (group[0], g))
+                for i in group:
+                    y_tiles[i, g] = (tile_, starts[group[0]], group[-1])
+
         def make_y(i):
             j0, w = starts[i], PIECES[i]
-            cols = slice(j0, j0 + w)
             per_bank = 512 // w
             for g in range(GROUPS):
-                y = sb([P, PACK, w], F32, "y%d_%d" % (i, g))
+                y, base, last = y_tiles[i, g]
                 for t0 in range(0, PACK, per_bank):
                     acc = bank(len(used))
-                    used.append(i)
                     for e in range(per_bank):
                         s0 = (g * PACK + t0 + e) * P
                         nc.tensor.matmul_mx(
@@ -236,26 +241,42 @@ def tile_list_face_transmissibility_kernel(
                             start=True,
                             stop=True,
                         )
-                    nc.scalar.copy(y[:, t0 : t0 + per_bank, :].rearrange("p e j -> p (e j)"), acc[:])
-                nc.sync.dma_start(
-                    out_0[g * KP : (g + 1) * KP, cols].rearrange("(p t) j -> p t j", t=PACK), y[:]
-                )
+                    dst = y[:, t0 : t0 + per_bank, j0 - base : j0 - base + w]
+                    src = acc[:].rearrange("p (e j) -> p e j", e=per_bank)
+                    if len(used) in VECTOR_BANKS:
+                        nc.vector.tensor_copy(dst, src)
+                    else:
+                        nc.scalar.copy(dst, src)
+                    used.append(i)
+                if i == last:
+                    nc.sync.dma_start(
+                        out_0[g * KP : (g + 1) * KP, base : j0 + w].rearrange("(p t) j -> p t j", t=PACK), y[:]
+                    )
+
+        def make_planes(i):
+            j0, w = starts[i], PIECES[i]
+            cols = slice(j0, j0 + w)
+            for g in range(GROUPS):
+                y, base, last = y_tiles[i, g]
                 y_bf = sb([P, w * PACK], BF16, "y_bf%d_%d" % (i, g))
                 nc.vector.tensor_copy(
                     y_bf[:].rearrange("p (c i t) -> p c t i", i=4, t=PACK),
-                    y[:].rearrange("p t (c i) -> p c t i", i=4),
+                    y[:, :, j0 - base : j0 - base + w].rearrange("p t (c i) -> p c t i", i=4),
                 )
                 nc.vector.quantize_mx(y_w[:, g, cols].bitcast(FP8X4), y_sc[:, g, cols], y_bf[:])
-            if i in WORD_STORES:
-                first = ([-1] + WORD_STORES)[WORD_STORES.index(i)] + 1
-                span = slice(starts[first], j0 + w)
-                nc.sync.dma_start(out_words[:, :, span], y_w[:, :, span])
+            for group in WORD_STORES:
+                if i == group[-1]:
+                    span = slice(starts[group[0]], j0 + w)
+                    nc.sync.dma_start(out_words[:, :, span], y_w[:, :, span])
 
-        make_h(0)
-        for i in range(len(PIECES)):
-            if i + 1 < len(PIECES):
-                make_h(i + 1)
-            make_y(i)
+        count = len(PIECES)
+        for step in range(-1, count + PLANE_LAG):
+            if step + 1 < count:
+                make_h(step + 1)
+            if 0 <= step < count:
+                make_y(step)
+            if 0 <= step - PLANE_LAG:
+                make_planes(step - PLANE_LAG)
 
         for q in range(4):
             nc.sync.dma_start(

@@ -24,9 +24,11 @@ GROUPS = N // KP
 CHUNK = 512
 CHUNKS = S // CHUNK
 PIECES = [128, 256, 256, 256, 128]
-Y_STORES = [[0], [1], [2], [3, 4]]
-WORD_STORES = [[0, 1], [2, 3, 4]]
-VECTOR_BANKS = (1, 3)
+Y_STORES = [[0], [1], [2], [3], [4]]
+WORD_STORES = [[0, 1, 2], [3], [4]]
+VECTOR_BANKS = (1, 3, 5)
+SCALAR_SQUARES = ()
+SCALAR_WEAVES = ((3, 1), (4, 1))
 PLANE_LAG = 2
 BANKS = 8
 
@@ -39,8 +41,8 @@ def tile_list_face_transmissibility_kernel(
         keep = ctx.enter_context(tc.tile_pool(name="keep", bufs=1))
         psum = ctx.enter_context(tc.psum_pool(name="psum", bufs=1))
 
-        def sb(shape, dtype, name):
-            return keep.tile(shape, dtype, name=name, align_bytes=64)
+        def sb(shape, dtype, name, tag=""):
+            return keep.tile(shape, dtype, name=name, tag=tag or name, align_bytes=64)
 
         def bank(b):
             return psum.tile([P, 512], F32, name="bank%d" % (b % BANKS))
@@ -52,14 +54,42 @@ def tile_list_face_transmissibility_kernel(
         nc.vector.memset(tab_sc[:].bitcast(I32), 0)
         v_sc1 = sb([P, S], U8, "v_sc1")
         nc.vector.memset(v_sc1[:].bitcast(I32), 0)
-        wr_sc_raw = sb([P, PASSES * H], U8, "wr_sc_raw")
+        wr_sc_raw = sb([P, PASSES * H], U8, "wr_sc_raw", "reused")
         nc.gpsimd.memset(wr_sc_raw[:].bitcast(I32), 0)
         wo_sc_raw = sb([P, N], U8, "wo_sc_raw")
         nc.gpsimd.memset(wo_sc_raw[:].bitcast(I32), 0)
 
+        warm = sb([P, 1], F32, "warm")
+        nc.gpsimd.memset(warm[:], 0.0)
+        warm_out = sb([P, 1], F32, "warm_out")
+        nc.scalar.activation(warm_out[:], warm[:], ACT.Exp)
+
+        wr_raw = sb([P, PASSES * 2 * H], U8, "wr_raw")
+        nc.sync.dma_start(
+            wr_raw[:].bitcast(I32).rearrange("p (a n) -> p a n", a=PASSES),
+            wr_words.bitcast(I32).rearrange("a p n -> p a n"),
+        )
+        mob_sb = sb([P, PACK], F32, "mob_sb")
+        nc.sync.dma_start(mob_sb[:], mob.rearrange("(p t) -> p t", t=PACK))
+        tab_sc_rows = tab_scales.rearrange("a (q r) n -> r q a n", r=4)
+        for r in range(4):
+            nc.sync.dma_start(tab_sc[r:P:16, :].bitcast(I32), tab_sc_rows[r].bitcast(I32))
         tab_w = [sb([P, T], I32, "tab_w%d" % a) for a in range(PASSES)]
-        for a in range(PASSES):
+
+        def load_table(a):
             nc.sync.dma_start(tab_w[a][:], tab_words[a].rearrange("p n t -> p (n t)").bitcast(I32))
+
+        load_table(0)
+        for q in range(4):
+            nc.sync.dma_start(
+                wr_sc_raw[32 * q : 32 * q + 4, :].bitcast(I32).rearrange("r (a n) -> r a n", a=PASSES),
+                wr_scales[:, 4 * q : 4 * q + 4, :].bitcast(I32).rearrange("a r n -> r a n"),
+            )
+        load_table(1)
+        v_sc0 = sb([P, S], U8, "v_sc0")
+        nc.vector.tensor_copy(v_sc0[:], tab_sc[:].indirect(offsets[:]))
+        nc.sync.dma_start(v_sc1[0:112, :].bitcast(I32), v_sc0[16:P, :].bitcast(I32))
+        v_sc = [v_sc0, v_sc1]
         wl_parts = [(0, 0, H), (1, 0, H)]
         wl_raw = []
         for a, c0, w in wl_parts:
@@ -75,30 +105,6 @@ def tile_list_face_transmissibility_kernel(
                 wo_sc_raw[32 * q : 32 * q + 4, :].bitcast(I32),
                 wo_scales[0, 4 * q : 4 * q + 4, :].bitcast(I32),
             )
-
-        wr_raw = sb([P, PASSES * 2 * H], U8, "wr_raw")
-        nc.scalar.dma_start(
-            wr_raw[:].bitcast(I32).rearrange("p (a n) -> p a n", a=PASSES),
-            wr_words.bitcast(I32).rearrange("a p n -> p a n"),
-        )
-        mob_sb = sb([P, PACK], F32, "mob_sb")
-        nc.scalar.dma_start(mob_sb[:], mob.rearrange("(p t) -> p t", t=PACK))
-        tab_sc_rows = tab_scales.rearrange("a (q r) n -> r q a n", r=4)
-        for r in range(4):
-            nc.scalar.dma_start(tab_sc[r:P:16, :].bitcast(I32), tab_sc_rows[r].bitcast(I32))
-        for q in range(4):
-            nc.scalar.dma_start(
-                wr_sc_raw[32 * q : 32 * q + 4, :].bitcast(I32).rearrange("r (a n) -> r a n", a=PASSES),
-                wr_scales[:, 4 * q : 4 * q + 4, :].bitcast(I32).rearrange("a r n -> r a n"),
-            )
-        v_sc0 = sb([P, S], U8, "v_sc0")
-        nc.vector.tensor_copy(v_sc0[:], tab_sc[:].indirect(offsets[:]))
-        nc.scalar.dma_start(v_sc1[0:112, :].bitcast(I32), v_sc0[16:P, :].bitcast(I32))
-        v_sc = [v_sc0, v_sc1]
-        warm = sb([P, 1], F32, "warm")
-        nc.gpsimd.memset(warm[:], 0.0)
-        warm_out = sb([P, 1], F32, "warm_out")
-        nc.scalar.activation(warm_out[:], warm[:], ACT.Exp)
 
         wr_w = sb([P, PASSES * 2 * H], U8, "wr_w")
         nc.vector.tensor_copy(
@@ -116,7 +122,7 @@ def tile_list_face_transmissibility_kernel(
         v_w = {}
         for a in range(PASSES):
             for c in range(CHUNKS):
-                t_ = sb([P, CHUNK], U32, "v_w%d_%d" % (a, c))
+                t_ = sb([P, CHUNK], U32, "v_w%d_%d" % (a, c), "reused" if (a, c) == (0, 1) else "")
                 cols = CHUNK // 16
                 nc.vector.tensor_copy(
                     t_[:], tab_w[a][:].bitcast(U32).indirect(offsets[:, c * cols : (c + 1) * cols])
@@ -157,12 +163,18 @@ def tile_list_face_transmissibility_kernel(
         wl_w = [sb([P, H], U32, "wl_w%d" % a) for a in range(PASSES)]
         wl_sc = [sb([P, H], U8, "wl_sc%d" % a) for a in range(PASSES)]
         for (a, c0, w), raw in zip(wl_parts, wl_raw):
-            nc.vector.tensor_copy(
-                wl_bf[a][:].rearrange("p (t m j) -> p m j t", t=PACK, j=PACK)[:, c0 // PACK : (c0 + w) // PACK],
-                raw[:].rearrange("p j (m t) -> p m j t", t=PACK),
-            )
-            if c0 + w == H:
-                nc.vector.quantize_mx(wl_w[a][:].bitcast(FP8X4), wl_sc[a][:], wl_bf[a][:])
+            halves = 1 if a == 0 else 2
+            span = PACK // halves
+            for t0 in range(0, PACK, span):
+                nc.vector.tensor_copy(
+                    wl_bf[a][:].rearrange("p (t m j) -> p m j t", t=PACK, j=PACK)[:, :, :, t0 : t0 + span],
+                    raw[:].rearrange("p j (m t) -> p m j t", t=PACK)[:, :, :, t0 : t0 + span],
+                )
+                nc.vector.quantize_mx(
+                    wl_w[a][:, t0 * P : (t0 + span) * P].bitcast(FP8X4),
+                    wl_sc[a][:, t0 * P : (t0 + span) * P],
+                    wl_bf[a][:, t0 * KP : (t0 + span) * KP],
+                )
 
         rl = first_stage(
             lambda a, t: wl_w[a][:, t * P : (t + 1) * P].bitcast(FP8X4),
@@ -208,9 +220,11 @@ def tile_list_face_transmissibility_kernel(
                 )
             h_bf = sb([P, w * PACK], BF16, "h_bf%d" % i)
             by_line = root[:].rearrange("p t (c i) -> p c t i", i=4)
-            nc.vector.tensor_tensor(
-                h_bf[:].rearrange("p (c i t) -> p c t i", i=4, t=PACK), by_line, by_line, ALU.mult
-            )
+            woven = h_bf[:].rearrange("p (c i t) -> p c t i", i=4, t=PACK)
+            if i in SCALAR_SQUARES:
+                nc.scalar.activation(woven, by_line, ACT.Square)
+            else:
+                nc.vector.tensor_tensor(woven, by_line, by_line, ALU.mult)
             h_w[i] = sb([P, w], U32, "h_w%d" % i)
             h_sc[i] = sb([P, w], U8, "h_sc%d" % i)
             nc.vector.quantize_mx(h_w[i][:].bitcast(FP8X4), h_sc[i][:], h_bf[:])
@@ -259,7 +273,8 @@ def tile_list_face_transmissibility_kernel(
             for g in range(GROUPS):
                 y, base, last = y_tiles[i, g]
                 y_bf = sb([P, w * PACK], BF16, "y_bf%d_%d" % (i, g))
-                nc.vector.tensor_copy(
+                weave = nc.scalar.copy if (i, g) in SCALAR_WEAVES else nc.vector.tensor_copy
+                weave(
                     y_bf[:].rearrange("p (c i t) -> p c t i", i=4, t=PACK),
                     y[:, :, j0 - base : j0 - base + w].rearrange("p t (c i) -> p c t i", i=4),
                 )

@@ -23,14 +23,14 @@ PASSES = K // KP
 GROUPS = N // KP
 CHUNK = 512
 CHUNKS = S // CHUNK
-PIECES = [128, 256, 256, 256, 128]
-Y_STORES = [[0], [1], [2], [3], [4]]
-WORD_STORES = [[0, 1, 2], [3], [4]]
-VECTOR_BANKS = (1, 3, 5)
-SCALAR_SQUARES = ()
-SCALAR_WEAVES = ((3, 1), (4, 1))
-PLANE_LAG = 2
+PIECES = [128, 128, 256, 512]
+VECTOR_BANKS = (0, 1)
+SCALAR_SQUARES = 2
+PLANE_LAG = 1
+PLANE_UNIT = 256
 BANKS = 8
+TABLE_HEAD = 1024
+MOVES_AHEAD = 6
 
 
 def tile_list_face_transmissibility_kernel(
@@ -52,44 +52,45 @@ def tile_list_face_transmissibility_kernel(
 
         tab_sc = sb([P, T], U8, "tab_sc")
         nc.vector.memset(tab_sc[:].bitcast(I32), 0)
-        v_sc1 = sb([P, S], U8, "v_sc1")
-        nc.vector.memset(v_sc1[:].bitcast(I32), 0)
         wr_sc_raw = sb([P, PASSES * H], U8, "wr_sc_raw", "reused")
-        nc.gpsimd.memset(wr_sc_raw[:].bitcast(I32), 0)
+        nc.vector.memset(wr_sc_raw[:].bitcast(I32), 0)
+        v_sc = [sb([P, S], U8, "v_sc%d" % a) for a in range(PASSES)]
+        for a in range(PASSES):
+            nc.vector.memset(v_sc[a][:].bitcast(I32), 0)
         wo_sc_raw = sb([P, N], U8, "wo_sc_raw")
-        nc.gpsimd.memset(wo_sc_raw[:].bitcast(I32), 0)
-
-        warm = sb([P, 1], F32, "warm")
-        nc.gpsimd.memset(warm[:], 0.0)
-        warm_out = sb([P, 1], F32, "warm_out")
-        nc.scalar.activation(warm_out[:], warm[:], ACT.Exp)
+        nc.vector.memset(wo_sc_raw[:].bitcast(I32), 0)
 
         wr_raw = sb([P, PASSES * 2 * H], U8, "wr_raw")
         nc.sync.dma_start(
             wr_raw[:].bitcast(I32).rearrange("p (a n) -> p a n", a=PASSES),
             wr_words.bitcast(I32).rearrange("a p n -> p a n"),
         )
-        mob_sb = sb([P, PACK], F32, "mob_sb")
-        nc.sync.dma_start(mob_sb[:], mob.rearrange("(p t) -> p t", t=PACK))
-        tab_sc_rows = tab_scales.rearrange("a (q r) n -> r q a n", r=4)
-        for r in range(4):
-            nc.sync.dma_start(tab_sc[r:P:16, :].bitcast(I32), tab_sc_rows[r].bitcast(I32))
         tab_w = [sb([P, T], I32, "tab_w%d" % a) for a in range(PASSES)]
 
-        def load_table(a):
-            nc.sync.dma_start(tab_w[a][:], tab_words[a].rearrange("p n t -> p (n t)").bitcast(I32))
+        def load_table(a, c0, c1):
+            nc.sync.dma_start(
+                tab_w[a][:, c0:c1], tab_words[a].rearrange("p n t -> p (n t)").bitcast(I32)[:, c0:c1]
+            )
 
-        load_table(0)
+        load_table(0, 0, TABLE_HEAD)
+        nc.sync.dma_start(tab_sc[0:P:4, :].bitcast(I32), tab_scales.rearrange("a q n -> (a q) n").bitcast(I32))
         for q in range(4):
             nc.sync.dma_start(
                 wr_sc_raw[32 * q : 32 * q + 4, :].bitcast(I32).rearrange("r (a n) -> r a n", a=PASSES),
                 wr_scales[:, 4 * q : 4 * q + 4, :].bitcast(I32).rearrange("a r n -> r a n"),
             )
-        load_table(1)
-        v_sc0 = sb([P, S], U8, "v_sc0")
-        nc.vector.tensor_copy(v_sc0[:], tab_sc[:].indirect(offsets[:]))
-        nc.sync.dma_start(v_sc1[0:112, :].bitcast(I32), v_sc0[16:P, :].bitcast(I32))
-        v_sc = [v_sc0, v_sc1]
+        load_table(0, TABLE_HEAD, T)
+        load_table(1, 0, T // 2)
+        picked_sc = sb([P, S], U8, "picked_sc")
+        nc.vector.tensor_copy(picked_sc[:], tab_sc[:].indirect(offsets[:]))
+        for move in range(4 * PASSES):
+            if move == MOVES_AHEAD:
+                load_table(1, T // 2, T)
+            a, q = divmod(move, 4)
+            nc.sync.dma_start(
+                v_sc[a][32 * q : 32 * q + 4, :].bitcast(I32),
+                picked_sc[16 * move : 16 * move + 16 : 4, :].bitcast(I32),
+            )
         wl_parts = [(0, 0, H), (1, 0, H)]
         wl_raw = []
         for a, c0, w in wl_parts:
@@ -98,6 +99,8 @@ def tile_list_face_transmissibility_kernel(
                 t_[:], wl[a * KP : (a + 1) * KP, c0 : c0 + w].rearrange("(p j) c -> p j c", j=PACK)
             )
             wl_raw.append(t_)
+        mob_sb = sb([P, PACK], F32, "mob_sb")
+        nc.sync.dma_start(mob_sb[:], mob.rearrange("(p t) -> p t", t=PACK))
         wo_raw = sb([P, N], I32, "wo_raw")
         nc.sync.dma_start(wo_raw[:], wo_words[0].rearrange("p n t -> p (n t)").bitcast(I32))
         for q in range(4):
@@ -131,9 +134,9 @@ def tile_list_face_transmissibility_kernel(
 
         def first_stage(lhs, lhs_scale, name, order):
             acc = {}
-            for a, c in order:
+            for a in range(PASSES):
                 if True:
-                    for t in range(PACK):
+                    for c, t in order:
                         if a == 0:
                             acc[c, t] = bank(c * PACK + t)
                         nc.tensor.matmul_mx(
@@ -146,26 +149,23 @@ def tile_list_face_transmissibility_kernel(
                             stop=(a == PASSES - 1),
                         )
             res = {}
-            for c in range(CHUNKS):
-                for t in range(PACK):
-                    res[c, t] = sb([P, CHUNK], F32, "%s%d_%d" % (name, c, t))
-                    nc.scalar.activation(res[c, t][:], acc[c, t][:], ACT.Exp)
+            for c, t in order:
+                res[c, t] = sb([P, CHUNK], F32, "%s%d_%d" % (name, c, t))
+                nc.scalar.activation(res[c, t][:], acc[c, t][:], ACT.Exp)
             return res
 
         rr = first_stage(
             lambda a, t: wr_w[:, (a * PACK + t) * 2 * P : (a * PACK + t + 1) * 2 * P].bitcast(FP4X4),
             lambda a, t: wr_sc[:, (a * PACK + t) * P : (a * PACK + t + 1) * P],
             "rr",
-            [(a, c) for a in range(PASSES) for c in range(CHUNKS)],
+            [(c, t) for c in range(CHUNKS) for t in range(PACK)],
         )
 
         wl_bf = [sb([P, PACK * H], BF16, "wl_bf%d" % a) for a in range(PASSES)]
         wl_w = [sb([P, H], U32, "wl_w%d" % a) for a in range(PASSES)]
         wl_sc = [sb([P, H], U8, "wl_sc%d" % a) for a in range(PASSES)]
         for (a, c0, w), raw in zip(wl_parts, wl_raw):
-            halves = 1 if a == 0 else 2
-            span = PACK // halves
-            for t0 in range(0, PACK, span):
+            for t0, span in ((0, 2), (2, 2)) if a == 0 else ((0, 1), (1, 1), (2, 2)):
                 nc.vector.tensor_copy(
                     wl_bf[a][:].rearrange("p (t m j) -> p m j t", t=PACK, j=PACK)[:, :, :, t0 : t0 + span],
                     raw[:].rearrange("p j (m t) -> p m j t", t=PACK)[:, :, :, t0 : t0 + span],
@@ -180,12 +180,12 @@ def tile_list_face_transmissibility_kernel(
             lambda a, t: wl_w[a][:, t * P : (t + 1) * P].bitcast(FP8X4),
             lambda a, t: wl_sc[a][:, t * P : (t + 1) * P],
             "rl",
-            [(a, c) for c in range(CHUNKS) for a in range(PASSES)],
+            [(c, t) for t in range(PACK) for c in range(CHUNKS)],
         )
 
         total = [sb([P, S], F32, "total%d" % t) for t in range(PACK)]
-        for c in range(CHUNKS):
-            for t in range(PACK):
+        for t in range(PACK):
+            for c in range(CHUNKS):
                 nc.vector.tensor_tensor(
                     total[t][:, c * CHUNK : (c + 1) * CHUNK], rl[c, t][:], rr[c, t][:], ALU.add
                 )
@@ -206,6 +206,7 @@ def tile_list_face_transmissibility_kernel(
         out_words = out_1.rearrange("g p n t -> p g (n t)").bitcast(I32)
         starts = [sum(PIECES[:i]) for i in range(len(PIECES) + 1)]
         h_w, h_sc = {}, {}
+        last = len(PIECES) - 1
         used = []
 
         def make_h(i):
@@ -218,30 +219,32 @@ def tile_list_face_transmissibility_kernel(
                     ACT.Abs_reciprocal_sqrt,
                     scale=inv_mob[:, t : t + 1],
                 )
-            h_bf = sb([P, w * PACK], BF16, "h_bf%d" % i)
-            by_line = root[:].rearrange("p t (c i) -> p c t i", i=4)
-            woven = h_bf[:].rearrange("p (c i t) -> p c t i", i=4, t=PACK)
-            if i in SCALAR_SQUARES:
-                nc.scalar.activation(woven, by_line, ACT.Square)
-            else:
-                nc.vector.tensor_tensor(woven, by_line, by_line, ALU.mult)
+            h_bf = sb([P, w * PACK], BF16, "h_bf%d" % i, "h_bf0" if i == 1 else "")
+            for c0 in range(0, w, P):
+                by_line = root[:, :, c0 : c0 + P].rearrange("p t (c i) -> p c t i", i=4)
+                woven = h_bf[:, c0 * PACK : (c0 + P) * PACK].rearrange("p (c i t) -> p c t i", i=4, t=PACK)
+                if i == last and c0 < SCALAR_SQUARES * P:
+                    nc.scalar.activation(woven, by_line, ACT.Square)
+                else:
+                    nc.vector.tensor_tensor(woven, by_line, by_line, ALU.mult)
             h_w[i] = sb([P, w], U32, "h_w%d" % i)
             h_sc[i] = sb([P, w], U8, "h_sc%d" % i)
-            nc.vector.quantize_mx(h_w[i][:].bitcast(FP8X4), h_sc[i][:], h_bf[:])
+            for c0 in range(0, w, P):
+                nc.vector.quantize_mx(
+                    h_w[i][:, c0 : c0 + P].bitcast(FP8X4),
+                    h_sc[i][:, c0 : c0 + P],
+                    h_bf[:, c0 * PACK : (c0 + P) * PACK],
+                )
 
         y_tiles = {}
-        for group in Y_STORES:
-            width = starts[group[-1] + 1] - starts[group[0]]
-            for g in range(GROUPS):
-                tile_ = sb([P, PACK, width], F32, "y%d_%d" % (group[0], g))
-                for i in group:
-                    y_tiles[i, g] = (tile_, starts[group[0]], group[-1])
 
         def make_y(i):
             j0, w = starts[i], PIECES[i]
             per_bank = 512 // w
             for g in range(GROUPS):
-                y, base, last = y_tiles[i, g]
+                y = sb([P, PACK, w], F32, "y%d_%d" % (i, g))
+                y_tiles[i, g] = y
+                rows = out_0[g * KP : (g + 1) * KP, j0 : j0 + w].rearrange("(p t) j -> p t j", t=PACK)
                 for t0 in range(0, PACK, per_bank):
                     acc = bank(len(used))
                     for e in range(per_bank):
@@ -255,34 +258,41 @@ def tile_list_face_transmissibility_kernel(
                             start=True,
                             stop=True,
                         )
-                    dst = y[:, t0 : t0 + per_bank, j0 - base : j0 - base + w]
+                    dst = y[:, t0 : t0 + per_bank, :]
                     src = acc[:].rearrange("p (e j) -> p e j", e=per_bank)
                     if len(used) in VECTOR_BANKS:
                         nc.vector.tensor_copy(dst, src)
                     else:
                         nc.scalar.copy(dst, src)
                     used.append(i)
-                if i == last:
-                    nc.sync.dma_start(
-                        out_0[g * KP : (g + 1) * KP, base : j0 + w].rearrange("(p t) j -> p t j", t=PACK), y[:]
-                    )
+                    if i == last:
+                        nc.sync.dma_start(rows[:, t0, :], y[:, t0, :])
+                if i < last:
+                    nc.sync.dma_start(rows, y[:])
 
         def make_planes(i):
             j0, w = starts[i], PIECES[i]
-            cols = slice(j0, j0 + w)
+            unit = min(w, PLANE_UNIT)
             for g in range(GROUPS):
-                y, base, last = y_tiles[i, g]
                 y_bf = sb([P, w * PACK], BF16, "y_bf%d_%d" % (i, g))
-                weave = nc.scalar.copy if (i, g) in SCALAR_WEAVES else nc.vector.tensor_copy
-                weave(
-                    y_bf[:].rearrange("p (c i t) -> p c t i", i=4, t=PACK),
-                    y[:, :, j0 - base : j0 - base + w].rearrange("p t (c i) -> p c t i", i=4),
-                )
-                nc.vector.quantize_mx(y_w[:, g, cols].bitcast(FP8X4), y_sc[:, g, cols], y_bf[:])
-            for group in WORD_STORES:
-                if i == group[-1]:
-                    span = slice(starts[group[0]], j0 + w)
-                    nc.sync.dma_start(out_words[:, :, span], y_w[:, :, span])
+                for c0 in range(0, w, unit):
+                    final = (i, g, c0 + unit) == (last, GROUPS - 1, w)
+                    weave = nc.scalar.copy if final else nc.vector.tensor_copy
+                    weave(
+                        y_bf[:, c0 * PACK : (c0 + unit) * PACK].rearrange("p (c i t) -> p c t i", i=4, t=PACK),
+                        y_tiles[i, g][:, :, c0 : c0 + unit].rearrange("p t (c i) -> p c t i", i=4),
+                    )
+                for c0 in range(0, w, unit):
+                    cols = slice(j0 + c0, j0 + c0 + unit)
+                    nc.vector.quantize_mx(
+                        y_w[:, g, cols].bitcast(FP8X4), y_sc[:, g, cols], y_bf[:, c0 * PACK : (c0 + unit) * PACK]
+                    )
+                    if (i, g) == (last, GROUPS - 1):
+                        nc.sync.dma_start(out_words[:, g, cols], y_w[:, g, cols])
+                if i == last and g < GROUPS - 1:
+                    nc.sync.dma_start(out_words[:, g, j0:], y_w[:, g, j0:])
+            if i == last - 1:
+                nc.sync.dma_start(out_words[:, :, : j0 + w], y_w[:, :, : j0 + w])
 
         count = len(PIECES)
         for step in range(-1, count + PLANE_LAG):

@@ -23,10 +23,8 @@ PASSES = K // KP
 GROUPS = N // KP
 CHUNK = 512
 CHUNKS = S // CHUNK
-PIECES = [128, 128, 256, 512]
-VECTOR_BANKS = (0, 1)
-SCALAR_SQUARES = 2
-PLANE_LAG = 1
+PIECES = [128, 384, 512]
+VECTOR_BANKS = (0,)
 PLANE_UNIT = 256
 BANKS = 8
 TABLE_HEAD = 1024
@@ -51,20 +49,16 @@ def tile_list_face_transmissibility_kernel(
         nc.sync.dma_start(offsets[:], offs)
 
         tab_sc = sb([P, T], U8, "tab_sc")
-        nc.vector.memset(tab_sc[:].bitcast(I32), 0)
         wr_sc_raw = sb([P, PASSES * H], U8, "wr_sc_raw", "reused")
         nc.vector.memset(wr_sc_raw[:].bitcast(I32), 0)
+        nc.vector.memset(tab_sc[32:64, :].bitcast(I32), 0)
+        nc.gpsimd.memset(tab_sc[64:128, :].bitcast(I32), 0)
         v_sc = [sb([P, S], U8, "v_sc%d" % a) for a in range(PASSES)]
         for a in range(PASSES):
             nc.vector.memset(v_sc[a][:].bitcast(I32), 0)
         wo_sc_raw = sb([P, N], U8, "wo_sc_raw")
         nc.vector.memset(wo_sc_raw[:].bitcast(I32), 0)
 
-        wr_raw = sb([P, PASSES * 2 * H], U8, "wr_raw")
-        nc.sync.dma_start(
-            wr_raw[:].bitcast(I32).rearrange("p (a n) -> p a n", a=PASSES),
-            wr_words.bitcast(I32).rearrange("a p n -> p a n"),
-        )
         tab_w = [sb([P, T], I32, "tab_w%d" % a) for a in range(PASSES)]
 
         def load_table(a, c0, c1):
@@ -72,25 +66,28 @@ def tile_list_face_transmissibility_kernel(
                 tab_w[a][:, c0:c1], tab_words[a].rearrange("p n t -> p (n t)").bitcast(I32)[:, c0:c1]
             )
 
-        load_table(0, 0, TABLE_HEAD)
-        nc.sync.dma_start(tab_sc[0:P:4, :].bitcast(I32), tab_scales.rearrange("a q n -> (a q) n").bitcast(I32))
+        nc.sync.dma_start(tab_sc[0:32, :].bitcast(I32), tab_scales.rearrange("a q n -> (a q) n").bitcast(I32))
+        load_table(0, 0, T // 2)
         for q in range(4):
             nc.sync.dma_start(
                 wr_sc_raw[32 * q : 32 * q + 4, :].bitcast(I32).rearrange("r (a n) -> r a n", a=PASSES),
                 wr_scales[:, 4 * q : 4 * q + 4, :].bitcast(I32).rearrange("a r n -> r a n"),
             )
-        load_table(0, TABLE_HEAD, T)
-        load_table(1, 0, T // 2)
+        wr_raw = sb([P, PASSES * 2 * H], U8, "wr_raw")
+        nc.sync.dma_start(
+            wr_raw[:].bitcast(I32).rearrange("p (a n) -> p a n", a=PASSES),
+            wr_words.bitcast(I32).rearrange("a p n -> p a n"),
+        )
+        load_table(0, T // 2, T)
         picked_sc = sb([P, S], U8, "picked_sc")
         nc.vector.tensor_copy(picked_sc[:], tab_sc[:].indirect(offsets[:]))
-        for move in range(4 * PASSES):
-            if move == MOVES_AHEAD:
-                load_table(1, T // 2, T)
-            a, q = divmod(move, 4)
-            nc.sync.dma_start(
-                v_sc[a][32 * q : 32 * q + 4, :].bitcast(I32),
-                picked_sc[16 * move : 16 * move + 16 : 4, :].bitcast(I32),
-            )
+        for a in range(PASSES):
+            for q in range(4):
+                row = 16 * a + 4 * q
+                nc.sync.dma_start(
+                    v_sc[a][32 * q : 32 * q + 4, :].bitcast(I32), picked_sc[row : row + 4, :].bitcast(I32)
+                )
+            load_table(1, a * T // 2, (a + 1) * T // 2)
         wl_parts = [(0, 0, H), (1, 0, H)]
         wl_raw = []
         for a, c0, w in wl_parts:
@@ -205,13 +202,16 @@ def tile_list_face_transmissibility_kernel(
         y_w = sb([P, GROUPS, S], I32, "y_w")
         out_words = out_1.rearrange("g p n t -> p g (n t)").bitcast(I32)
         starts = [sum(PIECES[:i]) for i in range(len(PIECES) + 1)]
-        h_w, h_sc = {}, {}
+        h_w = [sb([P, w], U32, "h_w%d" % i) for i, w in enumerate(PIECES)]
+        h_sc = [sb([P, w], U8, "h_sc%d" % i) for i, w in enumerate(PIECES)]
+        y_tiles = {
+            (i, g): sb([P, PACK, w], F32, "y%d_%d" % (i, g)) for i, w in enumerate(PIECES) for g in range(GROUPS)
+        }
         last = len(PIECES) - 1
         used = []
 
-        def make_h(i):
-            j0, w = starts[i], PIECES[i]
-            root = sb([P, PACK, w], F32, "root%d" % i)
+        def make_h(j0, w):
+            root = sb([P, PACK, w], F32, "root%d" % j0)
             for t in range(PACK):
                 nc.scalar.activation(
                     root[:, t, :],
@@ -219,89 +219,82 @@ def tile_list_face_transmissibility_kernel(
                     ACT.Abs_reciprocal_sqrt,
                     scale=inv_mob[:, t : t + 1],
                 )
-            h_bf = sb([P, w * PACK], BF16, "h_bf%d" % i, "h_bf0" if i == 1 else "")
             for c0 in range(0, w, P):
+                j = j0 + c0
+                i = max(k for k in range(len(PIECES)) if starts[k] <= j)
+                h_bf = sb([P, P * PACK], BF16, "h_bf%d" % j, "h_bf0" if j == P else "")
                 by_line = root[:, :, c0 : c0 + P].rearrange("p t (c i) -> p c t i", i=4)
-                woven = h_bf[:, c0 * PACK : (c0 + P) * PACK].rearrange("p (c i t) -> p c t i", i=4, t=PACK)
-                if i == last and c0 < SCALAR_SQUARES * P:
-                    nc.scalar.activation(woven, by_line, ACT.Square)
-                else:
-                    nc.vector.tensor_tensor(woven, by_line, by_line, ALU.mult)
-            h_w[i] = sb([P, w], U32, "h_w%d" % i)
-            h_sc[i] = sb([P, w], U8, "h_sc%d" % i)
-            for c0 in range(0, w, P):
-                nc.vector.quantize_mx(
-                    h_w[i][:, c0 : c0 + P].bitcast(FP8X4),
-                    h_sc[i][:, c0 : c0 + P],
-                    h_bf[:, c0 * PACK : (c0 + P) * PACK],
-                )
+                woven = h_bf[:].rearrange("p (c i t) -> p c t i", i=4, t=PACK)
+                nc.vector.tensor_tensor(woven, by_line, by_line, ALU.mult)
+                cols = slice(j - starts[i], j - starts[i] + P)
+                nc.vector.quantize_mx(h_w[i][:, cols].bitcast(FP8X4), h_sc[i][:, cols], h_bf[:])
 
-        y_tiles = {}
-
-        def make_y(i):
+        def make_y(i, g):
             j0, w = starts[i], PIECES[i]
             per_bank = 512 // w
-            for g in range(GROUPS):
-                y = sb([P, PACK, w], F32, "y%d_%d" % (i, g))
-                y_tiles[i, g] = y
-                rows = out_0[g * KP : (g + 1) * KP, j0 : j0 + w].rearrange("(p t) j -> p t j", t=PACK)
-                for t0 in range(0, PACK, per_bank):
-                    acc = bank(len(used))
-                    for e in range(per_bank):
-                        s0 = (g * PACK + t0 + e) * P
+            y = y_tiles[i, g]
+            rows = out_0[g * KP : (g + 1) * KP, j0 : j0 + w].rearrange("(p t) j -> p t j", t=PACK)
+            spans = [(0, w)] if w != 384 else [(0, 128), (128, 256)]
+            for t0 in range(0, PACK, per_bank):
+                acc = bank(len(used))
+                for e in range(per_bank):
+                    s0 = (g * PACK + t0 + e) * P
+                    for c0, n in spans:
                         nc.tensor.matmul_mx(
-                            acc[:, e * w : (e + 1) * w],
+                            acc[:, e * w + c0 : e * w + c0 + n],
                             lhsT=wo_w[:, s0 : s0 + P].bitcast(FP8X4),
                             lhsT_scale=wo_sc[:, s0 : s0 + P],
-                            rhs=h_w[i][:].bitcast(FP8X4),
-                            rhs_scale=h_sc[i][:],
+                            rhs=h_w[i][:, c0 : c0 + n].bitcast(FP8X4),
+                            rhs_scale=h_sc[i][:, c0 : c0 + n],
                             start=True,
                             stop=True,
                         )
-                    dst = y[:, t0 : t0 + per_bank, :]
-                    src = acc[:].rearrange("p (e j) -> p e j", e=per_bank)
-                    if len(used) in VECTOR_BANKS:
-                        nc.vector.tensor_copy(dst, src)
-                    else:
-                        nc.scalar.copy(dst, src)
-                    used.append(i)
-                    if i == last:
-                        nc.sync.dma_start(rows[:, t0, :], y[:, t0, :])
-                if i < last:
-                    nc.sync.dma_start(rows, y[:])
+                dst = y[:, t0 : t0 + per_bank, :]
+                src = acc[:, : per_bank * w].rearrange("p (e j) -> p e j", e=per_bank)
+                if len(used) in VECTOR_BANKS:
+                    nc.vector.tensor_copy(dst, src)
+                else:
+                    nc.scalar.copy(dst, src)
+                used.append(i)
+                nc.sync.dma_start(rows[:, t0 : t0 + per_bank, :], dst)
 
-        def make_planes(i):
+        def make_planes(i, g):
             j0, w = starts[i], PIECES[i]
-            unit = min(w, PLANE_UNIT)
-            for g in range(GROUPS):
-                y_bf = sb([P, w * PACK], BF16, "y_bf%d_%d" % (i, g))
-                for c0 in range(0, w, unit):
-                    final = (i, g, c0 + unit) == (last, GROUPS - 1, w)
-                    weave = nc.scalar.copy if final else nc.vector.tensor_copy
-                    weave(
-                        y_bf[:, c0 * PACK : (c0 + unit) * PACK].rearrange("p (c i t) -> p c t i", i=4, t=PACK),
-                        y_tiles[i, g][:, :, c0 : c0 + unit].rearrange("p t (c i) -> p c t i", i=4),
-                    )
-                for c0 in range(0, w, unit):
-                    cols = slice(j0 + c0, j0 + c0 + unit)
-                    nc.vector.quantize_mx(
-                        y_w[:, g, cols].bitcast(FP8X4), y_sc[:, g, cols], y_bf[:, c0 * PACK : (c0 + unit) * PACK]
-                    )
-                    if (i, g) == (last, GROUPS - 1):
-                        nc.sync.dma_start(out_words[:, g, cols], y_w[:, g, cols])
-                if i == last and g < GROUPS - 1:
-                    nc.sync.dma_start(out_words[:, g, j0:], y_w[:, g, j0:])
-            if i == last - 1:
-                nc.sync.dma_start(out_words[:, :, : j0 + w], y_w[:, :, : j0 + w])
+            units = [(c0, min(PLANE_UNIT, w - c0)) for c0 in range(0, w, PLANE_UNIT)]
+            y_bf = sb([P, w * PACK], BF16, "y_bf%d_%d" % (i, g))
+            for c0, unit in units:
+                final = (i, g, c0 + unit) == (last, GROUPS - 1, w)
+                weave = nc.scalar.copy if final else nc.vector.tensor_copy
+                weave(
+                    y_bf[:, c0 * PACK : (c0 + unit) * PACK].rearrange("p (c i t) -> p c t i", i=4, t=PACK),
+                    y_tiles[i, g][:, :, c0 : c0 + unit].rearrange("p t (c i) -> p c t i", i=4),
+                )
+            for c0, unit in units:
+                cols = slice(j0 + c0, j0 + c0 + unit)
+                nc.vector.quantize_mx(
+                    y_w[:, g, cols].bitcast(FP8X4), y_sc[:, g, cols], y_bf[:, c0 * PACK : (c0 + unit) * PACK]
+                )
+            if (i, g) == (last - 1, 1):
+                nc.sync.dma_start(out_words[:, g, : j0 + w], y_w[:, g, : j0 + w])
+            if (i, g) == (last, 0):
+                nc.sync.dma_start(out_words[:, g, :], y_w[:, g, :])
+            if (i, g) == (last, 1):
+                nc.sync.dma_start(out_words[:, g, j0:], y_w[:, g, j0:])
 
-        count = len(PIECES)
-        for step in range(-1, count + PLANE_LAG):
-            if step + 1 < count:
-                make_h(step + 1)
-            if 0 <= step < count:
-                make_y(step)
-            if 0 <= step - PLANE_LAG:
-                make_planes(step - PLANE_LAG)
+        make_h(0, 128)
+        make_h(128, 128)
+        make_h(256, 256)
+        make_y(0, 0)
+        make_y(0, 1)
+        make_h(512, 256)
+        make_y(1, 0)
+        make_h(768, 256)
+        make_y(1, 1)
+        make_y(2, 0)
+        make_y(2, 1)
+        for i in range(len(PIECES)):
+            for g in range(GROUPS):
+                make_planes(i, g)
 
         for q in range(4):
             nc.sync.dma_start(

@@ -24,7 +24,8 @@ GROUPS = N // KP
 CHUNK = 512
 CHUNKS = S // CHUNK
 PIECES = [128, 384, 512]
-VECTOR_BANKS = (0,)
+VECTOR_BANKS = (0, 2, 3, 13)
+SCALAR_SQUARES = (384, 896)
 PLANE_UNIT = 256
 BANKS = 8
 TABLE_HEAD = 1024
@@ -49,16 +50,20 @@ def tile_list_face_transmissibility_kernel(
         nc.sync.dma_start(offsets[:], offs)
 
         tab_sc = sb([P, T], U8, "tab_sc")
+        nc.vector.memset(tab_sc[:].bitcast(I32), 0)
         wr_sc_raw = sb([P, PASSES * H], U8, "wr_sc_raw", "reused")
         nc.vector.memset(wr_sc_raw[:].bitcast(I32), 0)
-        nc.vector.memset(tab_sc[32:64, :].bitcast(I32), 0)
-        nc.gpsimd.memset(tab_sc[64:128, :].bitcast(I32), 0)
         v_sc = [sb([P, S], U8, "v_sc%d" % a) for a in range(PASSES)]
         for a in range(PASSES):
             nc.vector.memset(v_sc[a][:].bitcast(I32), 0)
         wo_sc_raw = sb([P, N], U8, "wo_sc_raw")
         nc.vector.memset(wo_sc_raw[:].bitcast(I32), 0)
 
+        wr_raw = sb([P, PASSES * 2 * H], U8, "wr_raw")
+        nc.sync.dma_start(
+            wr_raw[:].bitcast(I32).rearrange("p (a n) -> p a n", a=PASSES),
+            wr_words.bitcast(I32).rearrange("a p n -> p a n"),
+        )
         tab_w = [sb([P, T], I32, "tab_w%d" % a) for a in range(PASSES)]
 
         def load_table(a, c0, c1):
@@ -66,28 +71,25 @@ def tile_list_face_transmissibility_kernel(
                 tab_w[a][:, c0:c1], tab_words[a].rearrange("p n t -> p (n t)").bitcast(I32)[:, c0:c1]
             )
 
-        nc.sync.dma_start(tab_sc[0:32, :].bitcast(I32), tab_scales.rearrange("a q n -> (a q) n").bitcast(I32))
-        load_table(0, 0, T // 2)
+        load_table(0, 0, TABLE_HEAD)
+        nc.sync.dma_start(tab_sc[0:P:4, :].bitcast(I32), tab_scales.rearrange("a q n -> (a q) n").bitcast(I32))
         for q in range(4):
             nc.sync.dma_start(
                 wr_sc_raw[32 * q : 32 * q + 4, :].bitcast(I32).rearrange("r (a n) -> r a n", a=PASSES),
                 wr_scales[:, 4 * q : 4 * q + 4, :].bitcast(I32).rearrange("a r n -> r a n"),
             )
-        wr_raw = sb([P, PASSES * 2 * H], U8, "wr_raw")
-        nc.sync.dma_start(
-            wr_raw[:].bitcast(I32).rearrange("p (a n) -> p a n", a=PASSES),
-            wr_words.bitcast(I32).rearrange("a p n -> p a n"),
-        )
-        load_table(0, T // 2, T)
+        load_table(0, TABLE_HEAD, T)
+        load_table(1, 0, T // 2)
         picked_sc = sb([P, S], U8, "picked_sc")
         nc.vector.tensor_copy(picked_sc[:], tab_sc[:].indirect(offsets[:]))
-        for a in range(PASSES):
-            for q in range(4):
-                row = 16 * a + 4 * q
-                nc.sync.dma_start(
-                    v_sc[a][32 * q : 32 * q + 4, :].bitcast(I32), picked_sc[row : row + 4, :].bitcast(I32)
-                )
-            load_table(1, a * T // 2, (a + 1) * T // 2)
+        for move in range(4 * PASSES):
+            if move == MOVES_AHEAD:
+                load_table(1, T // 2, T)
+            a, q = divmod(move, 4)
+            nc.sync.dma_start(
+                v_sc[a][32 * q : 32 * q + 4, :].bitcast(I32),
+                picked_sc[16 * move : 16 * move + 16 : 4, :].bitcast(I32),
+            )
         wl_parts = [(0, 0, H), (1, 0, H)]
         wl_raw = []
         for a, c0, w in wl_parts:
@@ -210,7 +212,10 @@ def tile_list_face_transmissibility_kernel(
         last = len(PIECES) - 1
         used = []
 
-        def make_h(j0, w):
+        roots = {}
+        h_bf = {}
+
+        def make_roots(j0, w):
             root = sb([P, PACK, w], F32, "root%d" % j0)
             for t in range(PACK):
                 nc.scalar.activation(
@@ -220,14 +225,21 @@ def tile_list_face_transmissibility_kernel(
                     scale=inv_mob[:, t : t + 1],
                 )
             for c0 in range(0, w, P):
-                j = j0 + c0
-                i = max(k for k in range(len(PIECES)) if starts[k] <= j)
-                h_bf = sb([P, P * PACK], BF16, "h_bf%d" % j, "h_bf0" if j == P else "")
-                by_line = root[:, :, c0 : c0 + P].rearrange("p t (c i) -> p c t i", i=4)
-                woven = h_bf[:].rearrange("p (c i t) -> p c t i", i=4, t=PACK)
+                roots[j0 + c0] = root[:, :, c0 : c0 + P]
+
+        def square(j):
+            h_bf[j] = sb([P, P * PACK], BF16, "h_bf%d" % j, "h_bf0" if j == P else "")
+            by_line = roots[j].rearrange("p t (c i) -> p c t i", i=4)
+            woven = h_bf[j][:].rearrange("p (c i t) -> p c t i", i=4, t=PACK)
+            if j in SCALAR_SQUARES:
+                nc.scalar.activation(woven, by_line, ACT.Square)
+            else:
                 nc.vector.tensor_tensor(woven, by_line, by_line, ALU.mult)
-                cols = slice(j - starts[i], j - starts[i] + P)
-                nc.vector.quantize_mx(h_w[i][:, cols].bitcast(FP8X4), h_sc[i][:, cols], h_bf[:])
+
+        def quantise(j):
+            i = max(k for k in range(len(PIECES)) if starts[k] <= j)
+            cols = slice(j - starts[i], j - starts[i] + P)
+            nc.vector.quantize_mx(h_w[i][:, cols].bitcast(FP8X4), h_sc[i][:, cols], h_bf[j][:])
 
         def make_y(i, g):
             j0, w = starts[i], PIECES[i]
@@ -281,14 +293,31 @@ def tile_list_face_transmissibility_kernel(
             if (i, g) == (last, 1):
                 nc.sync.dma_start(out_words[:, g, j0:], y_w[:, g, j0:])
 
-        make_h(0, 128)
-        make_h(128, 128)
-        make_h(256, 256)
+        make_roots(0, 128)
+        square(0)
+        quantise(0)
+        make_roots(128, 128)
+        make_roots(256, 128)
+        make_roots(384, 128)
+        square(128)
+        square(256)
+        square(384)
         make_y(0, 0)
+        quantise(128)
+        quantise(256)
+        quantise(384)
         make_y(0, 1)
-        make_h(512, 256)
+        make_roots(512, 256)
+        make_roots(768, 256)
         make_y(1, 0)
-        make_h(768, 256)
+        square(512)
+        square(640)
+        quantise(512)
+        square(768)
+        quantise(640)
+        square(896)
+        quantise(768)
+        quantise(896)
         make_y(1, 1)
         make_y(2, 0)
         make_y(2, 1)
@@ -297,7 +326,8 @@ def tile_list_face_transmissibility_kernel(
                 make_planes(i, g)
 
         for q in range(4):
-            nc.sync.dma_start(
+            queue = nc.sync if q < 2 else nc.scalar
+            queue.dma_start(
                 out_2[:, 4 * q : 4 * q + 4, :].bitcast(I32).rearrange("g r n -> r g n"),
                 y_sc[32 * q : 32 * q + 4, :, :].bitcast(I32),
             )

@@ -28,8 +28,7 @@ VECTOR_BANKS = (0, 2, 3, 13)
 SCALAR_SQUARES = (384, 896)
 PLANE_UNIT = 256
 BANKS = 8
-TABLE_HEAD = 1024
-MOVES_AHEAD = 6
+TABLE_CUT = 1536
 
 
 def tile_list_face_transmissibility_kernel(
@@ -50,20 +49,16 @@ def tile_list_face_transmissibility_kernel(
         nc.sync.dma_start(offsets[:], offs)
 
         tab_sc = sb([P, T], U8, "tab_sc")
-        nc.vector.memset(tab_sc[:].bitcast(I32), 0)
         wr_sc_raw = sb([P, PASSES * H], U8, "wr_sc_raw", "reused")
         nc.vector.memset(wr_sc_raw[:].bitcast(I32), 0)
+        nc.vector.memset(tab_sc[32:64, :].bitcast(I32), 0)
+        nc.gpsimd.memset(tab_sc[64:128, :].bitcast(I32), 0)
         v_sc = [sb([P, S], U8, "v_sc%d" % a) for a in range(PASSES)]
         for a in range(PASSES):
             nc.vector.memset(v_sc[a][:].bitcast(I32), 0)
         wo_sc_raw = sb([P, N], U8, "wo_sc_raw")
         nc.vector.memset(wo_sc_raw[:].bitcast(I32), 0)
 
-        wr_raw = sb([P, PASSES * 2 * H], U8, "wr_raw")
-        nc.sync.dma_start(
-            wr_raw[:].bitcast(I32).rearrange("p (a n) -> p a n", a=PASSES),
-            wr_words.bitcast(I32).rearrange("a p n -> p a n"),
-        )
         tab_w = [sb([P, T], I32, "tab_w%d" % a) for a in range(PASSES)]
 
         def load_table(a, c0, c1):
@@ -71,25 +66,30 @@ def tile_list_face_transmissibility_kernel(
                 tab_w[a][:, c0:c1], tab_words[a].rearrange("p n t -> p (n t)").bitcast(I32)[:, c0:c1]
             )
 
-        load_table(0, 0, TABLE_HEAD)
-        nc.sync.dma_start(tab_sc[0:P:4, :].bitcast(I32), tab_scales.rearrange("a q n -> (a q) n").bitcast(I32))
+        nc.sync.dma_start(tab_sc[0:32, :].bitcast(I32), tab_scales.rearrange("a q n -> (a q) n").bitcast(I32))
+        load_table(0, 0, T // 2)
         for q in range(4):
             nc.sync.dma_start(
                 wr_sc_raw[32 * q : 32 * q + 4, :].bitcast(I32).rearrange("r (a n) -> r a n", a=PASSES),
                 wr_scales[:, 4 * q : 4 * q + 4, :].bitcast(I32).rearrange("a r n -> r a n"),
             )
-        load_table(0, TABLE_HEAD, T)
-        load_table(1, 0, T // 2)
+        wr_raw = sb([P, PASSES * 2 * H], U8, "wr_raw")
+        nc.sync.dma_start(
+            wr_raw[:].bitcast(I32).rearrange("p (a n) -> p a n", a=PASSES),
+            wr_words.bitcast(I32).rearrange("a p n -> p a n"),
+        )
+        load_table(0, T // 2, T)
+        load_table(1, 0, TABLE_CUT)
         picked_sc = sb([P, S], U8, "picked_sc")
         nc.vector.tensor_copy(picked_sc[:], tab_sc[:].indirect(offsets[:]))
-        for move in range(4 * PASSES):
-            if move == MOVES_AHEAD:
-                load_table(1, T // 2, T)
-            a, q = divmod(move, 4)
-            nc.sync.dma_start(
-                v_sc[a][32 * q : 32 * q + 4, :].bitcast(I32),
-                picked_sc[16 * move : 16 * move + 16 : 4, :].bitcast(I32),
-            )
+        for a in range(PASSES):
+            for q in range(4):
+                row = 16 * a + 4 * q
+                nc.sync.dma_start(
+                    v_sc[a][32 * q : 32 * q + 4, :].bitcast(I32), picked_sc[row : row + 4, :].bitcast(I32)
+                )
+            if a == 0:
+                load_table(1, TABLE_CUT, T)
         wl_parts = [(0, 0, H), (1, 0, H)]
         wl_raw = []
         for a, c0, w in wl_parts:
@@ -326,8 +326,7 @@ def tile_list_face_transmissibility_kernel(
                 make_planes(i, g)
 
         for q in range(4):
-            queue = nc.sync if q < 2 else nc.scalar
-            queue.dma_start(
+            nc.scalar.dma_start(
                 out_2[:, 4 * q : 4 * q + 4, :].bitcast(I32).rearrange("g r n -> r g n"),
                 y_sc[32 * q : 32 * q + 4, :, :].bitcast(I32),
             )

@@ -1,6 +1,7 @@
 from contextlib import ExitStack
 
 import concourse.mybir as mybir
+from concourse.masks import make_identity
 
 K, T, S, H, N = 1024, 4096, 1024, 512, 1024
 FLOPS = 2 * K * H * S * 2 + 2 * H * N * S
@@ -28,7 +29,10 @@ VECTOR_BANKS = (0, 2, 3, 13)
 SCALAR_SQUARES = (384, 896)
 PLANE_UNIT = 256
 BANKS = 8
-TABLE_CUT = 1536
+HALF = CHUNK // 2
+TABLE_CUT = 1280
+SCALE_ROW = (16, 80)
+TABLE_HEAD = 3072
 
 
 def tile_list_face_transmissibility_kernel(
@@ -39,8 +43,8 @@ def tile_list_face_transmissibility_kernel(
         keep = ctx.enter_context(tc.tile_pool(name="keep", bufs=1))
         psum = ctx.enter_context(tc.psum_pool(name="psum", bufs=1))
 
-        def sb(shape, dtype, name, tag=""):
-            return keep.tile(shape, dtype, name=name, tag=tag or name, align_bytes=64)
+        def sb(shape, dtype, name, tag="", align=64):
+            return keep.tile(shape, dtype, name=name, tag=tag or name, align_bytes=align)
 
         def bank(b):
             return psum.tile([P, 512], F32, name="bank%d" % (b % BANKS))
@@ -48,26 +52,29 @@ def tile_list_face_transmissibility_kernel(
         offsets = keep.tile([P, S // 16], U16, name="offsets")
         nc.sync.dma_start(offsets[:], offs)
 
-        tab_sc = sb([P, T], U8, "tab_sc")
+        tab_sc = sb([P, T], U8, "tab_sc", align=256)
         wr_sc_raw = sb([P, PASSES * H], U8, "wr_sc_raw", "reused")
         nc.vector.memset(wr_sc_raw[:].bitcast(I32), 0)
-        nc.vector.memset(tab_sc[32:64, :].bitcast(I32), 0)
-        nc.gpsimd.memset(tab_sc[64:128, :].bitcast(I32), 0)
+        for p0, p1 in ((0, 16), (32, 64)):
+            nc.vector.memset(tab_sc[p0:p1, :].bitcast(I32), 0)
+            nc.gpsimd.memset(tab_sc[64 + p0 : 64 + p1, :].bitcast(I32), 0)
         v_sc = [sb([P, S], U8, "v_sc%d" % a) for a in range(PASSES)]
         for a in range(PASSES):
             nc.vector.memset(v_sc[a][:].bitcast(I32), 0)
         wo_sc_raw = sb([P, N], U8, "wo_sc_raw")
         nc.vector.memset(wo_sc_raw[:].bitcast(I32), 0)
 
-        tab_w = [sb([P, T], I32, "tab_w%d" % a) for a in range(PASSES)]
+        tab_w = [sb([P, T], I32, "tab_w%d" % a, align=256) for a in range(PASSES)]
 
         def load_table(a, c0, c1):
             nc.sync.dma_start(
                 tab_w[a][:, c0:c1], tab_words[a].rearrange("p n t -> p (n t)").bitcast(I32)[:, c0:c1]
             )
 
-        nc.sync.dma_start(tab_sc[0:32, :].bitcast(I32), tab_scales.rearrange("a q n -> (a q) n").bitcast(I32))
-        load_table(0, 0, T // 2)
+        for a in range(PASSES):
+            queue = nc.scalar if a else nc.sync
+            queue.dma_start(tab_sc[SCALE_ROW[a] : SCALE_ROW[a] + 16, :].bitcast(I32), tab_scales[a].bitcast(I32))
+        load_table(0, 0, TABLE_HEAD)
         for q in range(4):
             nc.sync.dma_start(
                 wr_sc_raw[32 * q : 32 * q + 4, :].bitcast(I32).rearrange("r (a n) -> r a n", a=PASSES),
@@ -78,30 +85,28 @@ def tile_list_face_transmissibility_kernel(
             wr_raw[:].bitcast(I32).rearrange("p (a n) -> p a n", a=PASSES),
             wr_words.bitcast(I32).rearrange("a p n -> p a n"),
         )
-        load_table(0, T // 2, T)
+        load_table(0, TABLE_HEAD, T)
         load_table(1, 0, TABLE_CUT)
         picked_sc = sb([P, S], U8, "picked_sc")
         nc.vector.tensor_copy(picked_sc[:], tab_sc[:].indirect(offsets[:]))
         for a in range(PASSES):
             for q in range(4):
-                row = 16 * a + 4 * q
+                row = SCALE_ROW[a] + 4 * q
                 nc.sync.dma_start(
                     v_sc[a][32 * q : 32 * q + 4, :].bitcast(I32), picked_sc[row : row + 4, :].bitcast(I32)
                 )
             if a == 0:
                 load_table(1, TABLE_CUT, T)
-        wl_parts = [(0, 0, H), (1, 0, H)]
+        wl_parts = [(0, 0, PACK), (1, 0, 2), (1, 2, PACK)]
         wl_raw = []
-        for a, c0, w in wl_parts:
-            t_ = sb([P, PACK, w], F32, "wl_raw%d_%d" % (a, c0))
+        for a, r0, r1 in wl_parts:
+            t_ = sb([P, r1 - r0, H], F32, "wl_raw%d_%d" % (a, r0), align=256)
             nc.sync.dma_start(
-                t_[:], wl[a * KP : (a + 1) * KP, c0 : c0 + w].rearrange("(p j) c -> p j c", j=PACK)
+                t_[:], wl[a * KP : (a + 1) * KP, :].rearrange("(p j) c -> p j c", j=PACK)[:, r0:r1, :]
             )
             wl_raw.append(t_)
         mob_sb = sb([P, PACK], F32, "mob_sb")
         nc.sync.dma_start(mob_sb[:], mob.rearrange("(p t) -> p t", t=PACK))
-        wo_raw = sb([P, N], I32, "wo_raw")
-        nc.sync.dma_start(wo_raw[:], wo_words[0].rearrange("p n t -> p (n t)").bitcast(I32))
         for q in range(4):
             nc.sync.dma_start(
                 wo_sc_raw[32 * q : 32 * q + 4, :].bitcast(I32),
@@ -118,96 +123,154 @@ def tile_list_face_transmissibility_kernel(
             wr_sc[:].rearrange("p (a t m) -> p a m t", a=PASSES, t=PACK),
             wr_sc_raw[:].rearrange("p (a m t) -> p a m t", a=PASSES, t=PACK),
         )
-        inv_mob = sb([P, PACK], F32, "inv_mob")
-        nc.vector.reciprocal(inv_mob[:], mob_sb[:])
 
         v_w = {}
         for a in range(PASSES):
             for c in range(CHUNKS):
                 t_ = sb([P, CHUNK], U32, "v_w%d_%d" % (a, c), "reused" if (a, c) == (0, 1) else "")
-                cols = CHUNK // 16
-                nc.vector.tensor_copy(
-                    t_[:], tab_w[a][:].bitcast(U32).indirect(offsets[:, c * cols : (c + 1) * cols])
-                )
+                cuts = (0, HALF, CHUNK) if (a, c) == (PASSES - 1, 0) else (0, CHUNK)
+                for j0, j1 in zip(cuts, cuts[1:]):
+                    nc.vector.tensor_copy(
+                        t_[:, j0:j1],
+                        tab_w[a][:].bitcast(U32).indirect(
+                            offsets[:, (c * CHUNK + j0) // 16 : (c * CHUNK + j1) // 16]
+                        ),
+                    )
                 v_w[a, c] = t_
 
-        def first_stage(lhs, lhs_scale, name, order):
+        ident = sb([P, P], F32, "ident")
+        make_identity(nc, ident[:])
+
+        def table(a, j0, w):
+            c, c0 = divmod(j0, CHUNK)
+            return v_w[a, c][:, c0 : c0 + w].bitcast(FP8X4), v_sc[a][:, j0 : j0 + w]
+
+        def first_stage(weight, name, order):
+            res = [sb([P, PACK, CHUNK], F32, "%s%d" % (name, c)) for c in range(CHUNKS)]
             acc = {}
             for a in range(PASSES):
-                if True:
-                    for c, t in order:
-                        if a == 0:
-                            acc[c, t] = bank(c * PACK + t)
+                for b, sums in order:
+                    if a == 0:
+                        acc[b] = bank(b)
+                    w = CHUNK // len(sums)
+                    for e, (r0, j0) in enumerate(sums):
+                        if j0 < CHUNK:
+                            lhs, rhs = weight(a, r0, P), table(a, j0, w)
+                        else:
+                            lhs, rhs = table(a, j0, P), weight(a, r0, w)
                         nc.tensor.matmul_mx(
-                            acc[c, t][:],
-                            lhsT=lhs(a, t),
-                            lhsT_scale=lhs_scale(a, t),
-                            rhs=v_w[a, c][:].bitcast(FP8X4),
-                            rhs_scale=v_sc[a][:, c * CHUNK : (c + 1) * CHUNK],
-                            start=(a == 0),
-                            stop=(a == PASSES - 1),
+                            acc[b][:, e * w : (e + 1) * w],
+                            lhsT=lhs[0],
+                            lhsT_scale=lhs[1],
+                            rhs=rhs[0],
+                            rhs_scale=rhs[1],
+                            start=(a == 0 and e == 0),
+                            stop=(a == PASSES - 1 and e == len(sums) - 1),
                         )
-            res = {}
-            for c, t in order:
-                res[c, t] = sb([P, CHUNK], F32, "%s%d_%d" % (name, c, t))
-                nc.scalar.activation(res[c, t][:], acc[c, t][:], ACT.Exp)
+            for b, sums in order:
+                r0, j0 = sums[0]
+                w = CHUNK // len(sums)
+                if j0 < CHUNK:
+                    dst = res[0][:, r0 // P : r0 // P + len(sums), j0 : j0 + w]
+                else:
+                    u = (j0 - CHUNK) // P
+                    dst = res[1][:, u : u + len(sums), r0 : r0 + w]
+                nc.scalar.activation(dst, acc[b][:].rearrange("p (e j) -> p e j", e=len(sums)), ACT.Exp)
             return res
 
         rr = first_stage(
-            lambda a, t: wr_w[:, (a * PACK + t) * 2 * P : (a * PACK + t + 1) * 2 * P].bitcast(FP4X4),
-            lambda a, t: wr_sc[:, (a * PACK + t) * P : (a * PACK + t + 1) * P],
+            lambda a, r0, w: (
+                wr_w[:, 2 * (a * H + r0) : 2 * (a * H + r0 + w)].bitcast(FP4X4),
+                wr_sc[:, a * H + r0 : a * H + r0 + w],
+            ),
             "rr",
-            [(c, t) for c in range(CHUNKS) for t in range(PACK)],
+            [(2 * u + k, [(2 * k * P, u * HALF), ((2 * k + 1) * P, u * HALF)]) for u in range(2) for k in range(2)]
+            + [(PACK + u, [(0, CHUNK + u * P)]) for u in range(PACK)],
         )
 
-        wl_bf = [sb([P, PACK * H], BF16, "wl_bf%d" % a) for a in range(PASSES)]
         wl_w = [sb([P, H], U32, "wl_w%d" % a) for a in range(PASSES)]
         wl_sc = [sb([P, H], U8, "wl_sc%d" % a) for a in range(PASSES)]
-        for (a, c0, w), raw in zip(wl_parts, wl_raw):
-            for t0, span in ((0, 2), (2, 2)) if a == 0 else ((0, 1), (1, 1), (2, 2)):
-                nc.vector.tensor_copy(
-                    wl_bf[a][:].rearrange("p (t m j) -> p m j t", t=PACK, j=PACK)[:, :, :, t0 : t0 + span],
-                    raw[:].rearrange("p j (m t) -> p m j t", t=PACK)[:, :, :, t0 : t0 + span],
-                )
-                nc.vector.quantize_mx(
-                    wl_w[a][:, t0 * P : (t0 + span) * P].bitcast(FP8X4),
-                    wl_sc[a][:, t0 * P : (t0 + span) * P],
-                    wl_bf[a][:, t0 * KP : (t0 + span) * KP],
-                )
 
+        def round_wl(part, bf, t0, span):
+            a, r0, r1 = wl_parts[part]
+            nc.vector.tensor_copy(
+                bf[:].rearrange("p (t m j) -> p m j t", t=span, j=PACK)[:, :, r0:r1, :],
+                wl_raw[part][:].rearrange("p j (m t) -> p m j t", t=PACK)[:, :, :, t0 : t0 + span],
+            )
+
+        def quantise_wl(a, bf, t0, span):
+            nc.vector.quantize_mx(
+                wl_w[a][:, t0 * P : (t0 + span) * P].bitcast(FP8X4),
+                wl_sc[a][:, t0 * P : (t0 + span) * P],
+                bf[:],
+            )
+
+        bf = sb([P, 2 * KP], BF16, "wl_bf00")
+        round_wl(0, bf, 0, 2)
+        quantise_wl(0, bf, 0, 2)
+        for t in range(2):
+            bf = sb([P, KP], BF16, "wl_bf1%d" % t, "wl_held%d" % t)
+            round_wl(1, bf, t, 1)
+            round_wl(2, bf, t, 1)
+            quantise_wl(1, bf, t, 1)
+        bf = sb([P, 2 * KP], BF16, "wl_bf02", "wl_held0")
+        round_wl(0, bf, 2, 2)
+        quantise_wl(0, bf, 2, 2)
+        bf = sb([P, 2 * KP], BF16, "wl_bf12", "wl_held1")
+        round_wl(1, bf, 2, 2)
+        round_wl(2, bf, 2, 2)
+        quantise_wl(1, bf, 2, 2)
+
+        rl_order = []
+        for h in range(2):
+            rl_order.extend([(4 * h + k, [((2 * h + k) * P, 0)]) for k in range(2)])
+            rl_order.extend(
+                [(4 * h + 2 + k, [(h * HALF, CHUNK + (2 * k + e) * P) for e in range(2)]) for k in range(2)]
+            )
         rl = first_stage(
-            lambda a, t: wl_w[a][:, t * P : (t + 1) * P].bitcast(FP8X4),
-            lambda a, t: wl_sc[a][:, t * P : (t + 1) * P],
-            "rl",
-            [(c, t) for t in range(PACK) for c in range(CHUNKS)],
+            lambda a, r0, w: (wl_w[a][:, r0 : r0 + w].bitcast(FP8X4), wl_sc[a][:, r0 : r0 + w]), "rl", rl_order
         )
 
-        total = [sb([P, S], F32, "total%d" % t) for t in range(PACK)]
+        inv_mob = sb([P, PACK], F32, "inv_mob", "wl_sc1")
+        nc.vector.reciprocal(inv_mob[:], mob_sb[:])
+        total = [[], []]
         for t in range(PACK):
-            for c in range(CHUNKS):
-                nc.vector.tensor_tensor(
-                    total[t][:, c * CHUNK : (c + 1) * CHUNK], rl[c, t][:], rr[c, t][:], ALU.add
-                )
+            total[0].append(sb([P, CHUNK], F32, "total%d" % t, "" if t else "wl_held1"))
+            nc.vector.tensor_tensor(total[0][t][:], rl[0][:, t, :], rr[0][:, t, :], ALU.add)
+        for t in range(PACK):
+            total[1].append(bank(PACK + t))
+            for n, term in enumerate((rr, rl)):
+                for u in range(PACK):
+                    nc.tensor.matmul(
+                        total[1][t][:, u * P : (u + 1) * P],
+                        lhsT=term[1][:, u, t * P : (t + 1) * P],
+                        rhs=ident[:],
+                        is_transpose=True,
+                        start=(n == 0 and u == 0),
+                        stop=(n == 1 and u == PACK - 1),
+                    )
 
+        wo_raw = sb([P, N], I32, "wo_raw", "wl_raw1_2", align=256)
+        nc.sync.dma_start(wo_raw[:], wo_words[0].rearrange("p n t -> p (n t)").bitcast(I32))
         wo_w = sb([P, N], I32, "wo_w")
         nc.vector.tensor_copy(
             wo_w[:].rearrange("p (g t m) -> p g m t", g=GROUPS, t=PACK),
             wo_raw[:].rearrange("p (g m t) -> p g m t", g=GROUPS, t=PACK),
         )
-        wo_sc = sb([P, N], U8, "wo_sc")
+        wo_sc = sb([P, N], U8, "wo_sc", "wl_raw1_2", align=256)
         nc.vector.tensor_copy(
             wo_sc[:].rearrange("p (g t m) -> p g m t", g=GROUPS, t=PACK),
             wo_sc_raw[:].rearrange("p (g m t) -> p g m t", g=GROUPS, t=PACK),
         )
 
         y_sc = sb([P, GROUPS, S], U8, "y_sc")
-        y_w = sb([P, GROUPS, S], I32, "y_w")
+        y_w = sb([P, GROUPS, S], I32, "y_w", align=256)
         out_words = out_1.rearrange("g p n t -> p g (n t)").bitcast(I32)
         starts = [sum(PIECES[:i]) for i in range(len(PIECES) + 1)]
         h_w = [sb([P, w], U32, "h_w%d" % i) for i, w in enumerate(PIECES)]
         h_sc = [sb([P, w], U8, "h_sc%d" % i) for i, w in enumerate(PIECES)]
         y_tiles = {
-            (i, g): sb([P, PACK, w], F32, "y%d_%d" % (i, g)) for i, w in enumerate(PIECES) for g in range(GROUPS)
+            (i, g): sb([P, PACK, w], F32, "y%d_%d" % (i, g), align=256) for i, w in enumerate(PIECES) for g in range(GROUPS)
         }
         last = len(PIECES) - 1
         used = []
@@ -220,7 +283,7 @@ def tile_list_face_transmissibility_kernel(
             for t in range(PACK):
                 nc.scalar.activation(
                     root[:, t, :],
-                    total[t][:, j0 : j0 + w],
+                    total[j0 // CHUNK][t][:, j0 % CHUNK : j0 % CHUNK + w],
                     ACT.Abs_reciprocal_sqrt,
                     scale=inv_mob[:, t : t + 1],
                 )
@@ -248,7 +311,7 @@ def tile_list_face_transmissibility_kernel(
             rows = out_0[g * KP : (g + 1) * KP, j0 : j0 + w].rearrange("(p t) j -> p t j", t=PACK)
             spans = [(0, w)] if w != 384 else [(0, 128), (128, 256)]
             for t0 in range(0, PACK, per_bank):
-                acc = bank(len(used))
+                acc = bank(len(used) + 2 if i == last else len(used) % 4)
                 for e in range(per_bank):
                     s0 = (g * PACK + t0 + e) * P
                     for c0, n in spans:
@@ -268,7 +331,10 @@ def tile_list_face_transmissibility_kernel(
                 else:
                     nc.scalar.copy(dst, src)
                 used.append(i)
-                nc.sync.dma_start(rows[:, t0 : t0 + per_bank, :], dst)
+                if i == 0 or (g == 0 and t0 < 2):
+                    nc.sync.dma_start(rows[:, t0 : t0 + per_bank, :], dst)
+                elif t0 % 2:
+                    nc.sync.dma_start(rows[:, t0 - 1 : t0 + 1, :], y[:, t0 - 1 : t0 + 1, :])
 
         def make_planes(i, g):
             j0, w = starts[i], PIECES[i]
@@ -286,12 +352,11 @@ def tile_list_face_transmissibility_kernel(
                 nc.vector.quantize_mx(
                     y_w[:, g, cols].bitcast(FP8X4), y_sc[:, g, cols], y_bf[:, c0 * PACK : (c0 + unit) * PACK]
                 )
-            if (i, g) == (last - 1, 1):
-                nc.sync.dma_start(out_words[:, g, : j0 + w], y_w[:, g, : j0 + w])
+                if (i, g) == (last, 1):
+                    first = 0 if c0 == 0 else cols.start
+                    nc.sync.dma_start(out_words[:, g, first : cols.stop], y_w[:, g, first : cols.stop])
             if (i, g) == (last, 0):
                 nc.sync.dma_start(out_words[:, g, :], y_w[:, g, :])
-            if (i, g) == (last, 1):
-                nc.sync.dma_start(out_words[:, g, j0:], y_w[:, g, j0:])
 
         make_roots(0, 128)
         square(0)

@@ -22,17 +22,23 @@ PACK = 4
 KP = P * PACK
 PASSES = K // KP
 GROUPS = N // KP
+BANKS = 8
+BANK = 512
 CHUNK = 512
 CHUNKS = S // CHUNK
+HALF = CHUNK // 2
+LIST_ROWS = 16
+QUADS, QUAD, LIVE = 4, 32, 4
+SCALE_ROWS = QUADS * LIVE
+LINE = 4
+ROW_ALIGN = 256
+SCALE_ROW = (16, 80)
+TABLE_HEAD = 3072
+TABLE_CUT = 1024
 PIECES = [128, 384, 512]
 VECTOR_BANKS = (0, 2, 3, 13)
 SCALAR_SQUARES = (384, 896)
 PLANE_UNIT = 256
-BANKS = 8
-HALF = CHUNK // 2
-TABLE_CUT = 1280
-SCALE_ROW = (16, 80)
-TABLE_HEAD = 3072
 
 
 def tile_list_face_transmissibility_kernel(
@@ -47,38 +53,42 @@ def tile_list_face_transmissibility_kernel(
             return keep.tile(shape, dtype, name=name, tag=tag or name, align_bytes=align)
 
         def bank(b):
-            return psum.tile([P, 512], F32, name="bank%d" % (b % BANKS))
+            return psum.tile([P, BANK], F32, name="bank%d" % (b % BANKS))
 
-        offsets = keep.tile([P, S // 16], U16, name="offsets")
+        def live(q):
+            return slice(QUAD * q, QUAD * q + LIVE)
+
+        offsets = keep.tile([P, S // LIST_ROWS], U16, name="offsets")
         nc.sync.dma_start(offsets[:], offs)
 
-        tab_sc = sb([P, T], U8, "tab_sc", align=256)
+        tab_sc = sb([P, T], U8, "tab_sc", align=ROW_ALIGN)
         wr_sc_raw = sb([P, PASSES * H], U8, "wr_sc_raw", "reused")
         nc.vector.memset(wr_sc_raw[:].bitcast(I32), 0)
-        for p0, p1 in ((0, 16), (32, 64)):
+        for p0, p1 in ((0, SCALE_ROW[0]), (QUAD, P // 2)):
             nc.vector.memset(tab_sc[p0:p1, :].bitcast(I32), 0)
-            nc.gpsimd.memset(tab_sc[64 + p0 : 64 + p1, :].bitcast(I32), 0)
+            nc.gpsimd.memset(tab_sc[P // 2 + p0 : P // 2 + p1, :].bitcast(I32), 0)
         v_sc = [sb([P, S], U8, "v_sc%d" % a) for a in range(PASSES)]
         for a in range(PASSES):
             nc.vector.memset(v_sc[a][:].bitcast(I32), 0)
         wo_sc_raw = sb([P, N], U8, "wo_sc_raw")
         nc.vector.memset(wo_sc_raw[:].bitcast(I32), 0)
 
-        tab_w = [sb([P, T], I32, "tab_w%d" % a, align=256) for a in range(PASSES)]
+        tab_w = [sb([P, T], I32, "tab_w%d" % a, align=ROW_ALIGN) for a in range(PASSES)]
 
         def load_table(a, c0, c1):
             nc.sync.dma_start(
                 tab_w[a][:, c0:c1], tab_words[a].rearrange("p n t -> p (n t)").bitcast(I32)[:, c0:c1]
             )
 
-        for a in range(PASSES):
-            queue = nc.scalar if a else nc.sync
-            queue.dma_start(tab_sc[SCALE_ROW[a] : SCALE_ROW[a] + 16, :].bitcast(I32), tab_scales[a].bitcast(I32))
+        for a, queue in enumerate((nc.sync, nc.scalar)):
+            queue.dma_start(
+                tab_sc[SCALE_ROW[a] : SCALE_ROW[a] + SCALE_ROWS, :].bitcast(I32), tab_scales[a].bitcast(I32)
+            )
         load_table(0, 0, TABLE_HEAD)
-        for q in range(4):
+        for q in range(QUADS):
             nc.sync.dma_start(
-                wr_sc_raw[32 * q : 32 * q + 4, :].bitcast(I32).rearrange("r (a n) -> r a n", a=PASSES),
-                wr_scales[:, 4 * q : 4 * q + 4, :].bitcast(I32).rearrange("a r n -> r a n"),
+                wr_sc_raw[live(q), :].bitcast(I32).rearrange("r (a n) -> r a n", a=PASSES),
+                wr_scales[:, LIVE * q : LIVE * (q + 1), :].bitcast(I32).rearrange("a r n -> r a n"),
             )
         wr_raw = sb([P, PASSES * 2 * H], U8, "wr_raw")
         nc.sync.dma_start(
@@ -87,36 +97,34 @@ def tile_list_face_transmissibility_kernel(
         )
         load_table(0, TABLE_HEAD, T)
         load_table(1, 0, TABLE_CUT)
+
         picked_sc = sb([P, S], U8, "picked_sc")
         nc.vector.tensor_copy(picked_sc[:], tab_sc[:].indirect(offsets[:]))
         for a in range(PASSES):
-            for q in range(4):
-                row = SCALE_ROW[a] + 4 * q
-                nc.sync.dma_start(
-                    v_sc[a][32 * q : 32 * q + 4, :].bitcast(I32), picked_sc[row : row + 4, :].bitcast(I32)
-                )
+            for q in range(QUADS):
+                row = SCALE_ROW[a] + LIVE * q
+                nc.sync.dma_start(v_sc[a][live(q), :].bitcast(I32), picked_sc[row : row + LIVE, :].bitcast(I32))
             if a == 0:
                 load_table(1, TABLE_CUT, T)
-        wl_parts = [(0, 0, PACK), (1, 0, 2), (1, 2, PACK)]
+
+        wl_parts = [(0, 0, PACK), (1, 0, PACK // 2), (1, PACK // 2, PACK)]
         wl_raw = []
         for a, r0, r1 in wl_parts:
-            t_ = sb([P, r1 - r0, H], F32, "wl_raw%d_%d" % (a, r0), align=256)
+            wl_raw.append(sb([P, r1 - r0, H], F32, "wl_raw%d_%d" % (a, r0), align=ROW_ALIGN))
             nc.sync.dma_start(
-                t_[:], wl[a * KP : (a + 1) * KP, :].rearrange("(p j) c -> p j c", j=PACK)[:, r0:r1, :]
+                wl_raw[-1][:], wl[a * KP : (a + 1) * KP, :].rearrange("(p r) c -> p r c", r=PACK)[:, r0:r1, :]
             )
-            wl_raw.append(t_)
         mob_sb = sb([P, PACK], F32, "mob_sb")
         nc.sync.dma_start(mob_sb[:], mob.rearrange("(p t) -> p t", t=PACK))
-        for q in range(4):
+        for q in range(QUADS):
             nc.sync.dma_start(
-                wo_sc_raw[32 * q : 32 * q + 4, :].bitcast(I32),
-                wo_scales[0, 4 * q : 4 * q + 4, :].bitcast(I32),
+                wo_sc_raw[live(q), :].bitcast(I32), wo_scales[0, LIVE * q : LIVE * (q + 1), :].bitcast(I32)
             )
 
         wr_w = sb([P, PASSES * 2 * H], U8, "wr_w")
         nc.vector.tensor_copy(
-            wr_w[:].rearrange("p (a t m b) -> p a m t b", a=PASSES, t=PACK, b=2),
-            wr_raw[:].rearrange("p (a m t b) -> p a m t b", a=PASSES, t=PACK, b=2),
+            wr_w[:].bitcast(U16).rearrange("p (a t m) -> p a m t", a=PASSES, t=PACK),
+            wr_raw[:].bitcast(U16).rearrange("p (a m t) -> p a m t", a=PASSES, t=PACK),
         )
         wr_sc = sb([P, PASSES * H], U8, "wr_sc")
         nc.vector.tensor_copy(
@@ -127,16 +135,11 @@ def tile_list_face_transmissibility_kernel(
         v_w = {}
         for a in range(PASSES):
             for c in range(CHUNKS):
-                t_ = sb([P, CHUNK], U32, "v_w%d_%d" % (a, c), "reused" if (a, c) == (0, 1) else "")
+                v_w[a, c] = sb([P, CHUNK], U32, "v_w%d_%d" % (a, c), "reused" if (a, c) == (0, 1) else "")
                 cuts = (0, HALF, CHUNK) if (a, c) == (PASSES - 1, 0) else (0, CHUNK)
                 for j0, j1 in zip(cuts, cuts[1:]):
-                    nc.vector.tensor_copy(
-                        t_[:, j0:j1],
-                        tab_w[a][:].bitcast(U32).indirect(
-                            offsets[:, (c * CHUNK + j0) // 16 : (c * CHUNK + j1) // 16]
-                        ),
-                    )
-                v_w[a, c] = t_
+                    listed = offsets[:, (c * CHUNK + j0) // LIST_ROWS : (c * CHUNK + j1) // LIST_ROWS]
+                    nc.vector.tensor_copy(v_w[a, c][:, j0:j1], tab_w[a][:].bitcast(U32).indirect(listed))
 
         ident = sb([P, P], F32, "ident")
         make_identity(nc, ident[:])
@@ -152,7 +155,7 @@ def tile_list_face_transmissibility_kernel(
                 for b, sums in order:
                     if a == 0:
                         acc[b] = bank(b)
-                    w = CHUNK // len(sums)
+                    w = BANK // len(sums)
                     for e, (r0, j0) in enumerate(sums):
                         if j0 < CHUNK:
                             lhs, rhs = weight(a, r0, P), table(a, j0, w)
@@ -169,149 +172,142 @@ def tile_list_face_transmissibility_kernel(
                         )
             for b, sums in order:
                 r0, j0 = sums[0]
-                w = CHUNK // len(sums)
+                w = BANK // len(sums)
                 if j0 < CHUNK:
                     dst = res[0][:, r0 // P : r0 // P + len(sums), j0 : j0 + w]
                 else:
-                    u = (j0 - CHUNK) // P
-                    dst = res[1][:, u : u + len(sums), r0 : r0 + w]
+                    block = (j0 - CHUNK) // P
+                    dst = res[1][:, block : block + len(sums), r0 : r0 + w]
                 nc.scalar.activation(dst, acc[b][:].rearrange("p (e j) -> p e j", e=len(sums)), ACT.Exp)
             return res
 
-        rr = first_stage(
-            lambda a, r0, w: (
-                wr_w[:, 2 * (a * H + r0) : 2 * (a * H + r0 + w)].bitcast(FP4X4),
-                wr_sc[:, a * H + r0 : a * H + r0 + w],
-            ),
-            "rr",
-            [(2 * u + k, [(2 * k * P, u * HALF), ((2 * k + 1) * P, u * HALF)]) for u in range(2) for k in range(2)]
-            + [(PACK + u, [(0, CHUNK + u * P)]) for u in range(PACK)],
-        )
+        def wr_columns(a, r0, w):
+            c0 = a * H + r0
+            return wr_w[:, 2 * c0 : 2 * (c0 + w)].bitcast(FP4X4), wr_sc[:, c0 : c0 + w]
+
+        rr_order = [
+            (2 * quarter + pair, [((2 * pair + e) * P, quarter * HALF) for e in range(2)])
+            for quarter in range(2)
+            for pair in range(2)
+        ]
+        rr_order.extend([(PACK + block, [(0, CHUNK + block * P)]) for block in range(PACK)])
+        rr = first_stage(wr_columns, "rr", rr_order)
 
         wl_w = [sb([P, H], U32, "wl_w%d" % a) for a in range(PASSES)]
         wl_sc = [sb([P, H], U8, "wl_sc%d" % a) for a in range(PASSES)]
 
-        def round_wl(part, bf, t0, span):
-            a, r0, r1 = wl_parts[part]
-            nc.vector.tensor_copy(
-                bf[:].rearrange("p (t m j) -> p m j t", t=span, j=PACK)[:, :, r0:r1, :],
-                wl_raw[part][:].rearrange("p j (m t) -> p m j t", t=PACK)[:, :, :, t0 : t0 + span],
-            )
+        def quantise_wl(a, t0, span, tag):
+            rounded = sb([P, span * KP], BF16, "wl_bf%d%d" % (a, t0), tag)
+            for raw, (part_pass, r0, r1) in zip(wl_raw, wl_parts):
+                if part_pass == a:
+                    nc.vector.tensor_copy(
+                        rounded[:].rearrange("p (t m r) -> p m r t", t=span, r=PACK)[:, :, r0:r1, :],
+                        raw[:].rearrange("p r (m t) -> p m r t", t=PACK)[:, :, :, t0 : t0 + span],
+                    )
+            cols = slice(t0 * P, (t0 + span) * P)
+            nc.vector.quantize_mx(wl_w[a][:, cols].bitcast(FP8X4), wl_sc[a][:, cols], rounded[:])
 
-        def quantise_wl(a, bf, t0, span):
-            nc.vector.quantize_mx(
-                wl_w[a][:, t0 * P : (t0 + span) * P].bitcast(FP8X4),
-                wl_sc[a][:, t0 * P : (t0 + span) * P],
-                bf[:],
-            )
-
-        bf = sb([P, 2 * KP], BF16, "wl_bf00")
-        round_wl(0, bf, 0, 2)
-        quantise_wl(0, bf, 0, 2)
+        quantise_wl(0, 0, 2, "")
         for t in range(2):
-            bf = sb([P, KP], BF16, "wl_bf1%d" % t, "wl_held%d" % t)
-            round_wl(1, bf, t, 1)
-            round_wl(2, bf, t, 1)
-            quantise_wl(1, bf, t, 1)
-        bf = sb([P, 2 * KP], BF16, "wl_bf02", "wl_held0")
-        round_wl(0, bf, 2, 2)
-        quantise_wl(0, bf, 2, 2)
-        bf = sb([P, 2 * KP], BF16, "wl_bf12", "wl_held1")
-        round_wl(1, bf, 2, 2)
-        round_wl(2, bf, 2, 2)
-        quantise_wl(1, bf, 2, 2)
+            quantise_wl(1, t, 1, "wl_held%d" % t)
+        for a in range(PASSES):
+            quantise_wl(a, 2, 2, "wl_held%d" % a)
+
+        def wl_columns(a, r0, w):
+            return wl_w[a][:, r0 : r0 + w].bitcast(FP8X4), wl_sc[a][:, r0 : r0 + w]
 
         rl_order = []
-        for h in range(2):
-            rl_order.extend([(4 * h + k, [((2 * h + k) * P, 0)]) for k in range(2)])
+        for pair in range(2):
+            rl_order.extend([(PACK * pair + e, [((2 * pair + e) * P, 0)]) for e in range(2)])
             rl_order.extend(
-                [(4 * h + 2 + k, [(h * HALF, CHUNK + (2 * k + e) * P) for e in range(2)]) for k in range(2)]
+                [
+                    (PACK * pair + 2 + two, [(pair * HALF, CHUNK + (2 * two + e) * P) for e in range(2)])
+                    for two in range(2)
+                ]
             )
-        rl = first_stage(
-            lambda a, r0, w: (wl_w[a][:, r0 : r0 + w].bitcast(FP8X4), wl_sc[a][:, r0 : r0 + w]), "rl", rl_order
-        )
+        rl = first_stage(wl_columns, "rl", rl_order)
 
         inv_mob = sb([P, PACK], F32, "inv_mob", "wl_sc1")
         nc.vector.reciprocal(inv_mob[:], mob_sb[:])
+
         total = [[], []]
         for t in range(PACK):
             total[0].append(sb([P, CHUNK], F32, "total%d" % t, "" if t else "wl_held1"))
             nc.vector.tensor_tensor(total[0][t][:], rl[0][:, t, :], rr[0][:, t, :], ALU.add)
         for t in range(PACK):
             total[1].append(bank(PACK + t))
-            for n, term in enumerate((rr, rl)):
-                for u in range(PACK):
+            for term in (rr, rl):
+                for block in range(PACK):
                     nc.tensor.matmul(
-                        total[1][t][:, u * P : (u + 1) * P],
-                        lhsT=term[1][:, u, t * P : (t + 1) * P],
+                        total[1][t][:, block * P : (block + 1) * P],
+                        lhsT=term[1][:, block, t * P : (t + 1) * P],
                         rhs=ident[:],
                         is_transpose=True,
-                        start=(n == 0 and u == 0),
-                        stop=(n == 1 and u == PACK - 1),
+                        start=(term is rr and block == 0),
+                        stop=(term is rl and block == PACK - 1),
                     )
 
-        wo_raw = sb([P, N], I32, "wo_raw", "wl_raw1_2", align=256)
+        wo_raw = sb([P, N], I32, "wo_raw", "wl_raw1_2", align=ROW_ALIGN)
         nc.sync.dma_start(wo_raw[:], wo_words[0].rearrange("p n t -> p (n t)").bitcast(I32))
         wo_w = sb([P, N], I32, "wo_w")
         nc.vector.tensor_copy(
             wo_w[:].rearrange("p (g t m) -> p g m t", g=GROUPS, t=PACK),
             wo_raw[:].rearrange("p (g m t) -> p g m t", g=GROUPS, t=PACK),
         )
-        wo_sc = sb([P, N], U8, "wo_sc", "wl_raw1_2", align=256)
+        wo_sc = sb([P, N], U8, "wo_sc", "wl_raw1_2", align=ROW_ALIGN)
         nc.vector.tensor_copy(
             wo_sc[:].rearrange("p (g t m) -> p g m t", g=GROUPS, t=PACK),
             wo_sc_raw[:].rearrange("p (g m t) -> p g m t", g=GROUPS, t=PACK),
         )
 
         y_sc = sb([P, GROUPS, S], U8, "y_sc")
-        y_w = sb([P, GROUPS, S], I32, "y_w", align=256)
+        y_w = sb([P, GROUPS, S], I32, "y_w", align=ROW_ALIGN)
         out_words = out_1.rearrange("g p n t -> p g (n t)").bitcast(I32)
-        starts = [sum(PIECES[:i]) for i in range(len(PIECES) + 1)]
+        starts = [sum(PIECES[:i]) for i in range(len(PIECES))]
         h_w = [sb([P, w], U32, "h_w%d" % i) for i, w in enumerate(PIECES)]
         h_sc = [sb([P, w], U8, "h_sc%d" % i) for i, w in enumerate(PIECES)]
         y_tiles = {
-            (i, g): sb([P, PACK, w], F32, "y%d_%d" % (i, g), align=256) for i, w in enumerate(PIECES) for g in range(GROUPS)
+            (i, g): sb([P, PACK, w], F32, "y%d_%d" % (i, g), align=ROW_ALIGN)
+            for i, w in enumerate(PIECES)
+            for g in range(GROUPS)
         }
         last = len(PIECES) - 1
         used = []
-
         roots = {}
         h_bf = {}
 
         def make_roots(j0, w):
+            c, c0 = divmod(j0, CHUNK)
             root = sb([P, PACK, w], F32, "root%d" % j0)
             for t in range(PACK):
                 nc.scalar.activation(
-                    root[:, t, :],
-                    total[j0 // CHUNK][t][:, j0 % CHUNK : j0 % CHUNK + w],
-                    ACT.Abs_reciprocal_sqrt,
-                    scale=inv_mob[:, t : t + 1],
+                    root[:, t, :], total[c][t][:, c0 : c0 + w], ACT.Abs_reciprocal_sqrt, scale=inv_mob[:, t : t + 1]
                 )
-            for c0 in range(0, w, P):
-                roots[j0 + c0] = root[:, :, c0 : c0 + P]
+            for u0 in range(0, w, P):
+                roots[j0 + u0] = root[:, :, u0 : u0 + P]
 
         def square(j):
             h_bf[j] = sb([P, P * PACK], BF16, "h_bf%d" % j, "h_bf0" if j == P else "")
-            by_line = roots[j].rearrange("p t (c i) -> p c t i", i=4)
-            woven = h_bf[j][:].rearrange("p (c i t) -> p c t i", i=4, t=PACK)
+            by_line = roots[j].rearrange("p t (c i) -> p c t i", i=LINE)
+            woven = h_bf[j][:].rearrange("p (c i t) -> p c t i", i=LINE, t=PACK)
             if j in SCALAR_SQUARES:
                 nc.scalar.activation(woven, by_line, ACT.Square)
             else:
                 nc.vector.tensor_tensor(woven, by_line, by_line, ALU.mult)
 
         def quantise(j):
-            i = max(k for k in range(len(PIECES)) if starts[k] <= j)
+            i = max(piece for piece, j0 in enumerate(starts) if j0 <= j)
             cols = slice(j - starts[i], j - starts[i] + P)
             nc.vector.quantize_mx(h_w[i][:, cols].bitcast(FP8X4), h_sc[i][:, cols], h_bf[j][:])
 
         def make_y(i, g):
             j0, w = starts[i], PIECES[i]
-            per_bank = 512 // w
+            per_bank = BANK // w
             y = y_tiles[i, g]
             rows = out_0[g * KP : (g + 1) * KP, j0 : j0 + w].rearrange("(p t) j -> p t j", t=PACK)
-            spans = [(0, w)] if w != 384 else [(0, 128), (128, 256)]
+            spans = [(0, P), (P, 2 * P)] if w == 3 * P else [(0, w)]
             for t0 in range(0, PACK, per_bank):
-                acc = bank(len(used) + 2 if i == last else len(used) % 4)
+                acc = bank(PACK * (1 - g) + t0 if i == last else len(used) % PACK)
                 for e in range(per_bank):
                     s0 = (g * PACK + t0 + e) * P
                     for c0, n in spans:
@@ -325,11 +321,8 @@ def tile_list_face_transmissibility_kernel(
                             stop=True,
                         )
                 dst = y[:, t0 : t0 + per_bank, :]
-                src = acc[:, : per_bank * w].rearrange("p (e j) -> p e j", e=per_bank)
-                if len(used) in VECTOR_BANKS:
-                    nc.vector.tensor_copy(dst, src)
-                else:
-                    nc.scalar.copy(dst, src)
+                empty = nc.vector.tensor_copy if len(used) in VECTOR_BANKS else nc.scalar.copy
+                empty(dst, acc[:, : per_bank * w].rearrange("p (e j) -> p e j", e=per_bank))
                 used.append(i)
                 if i == 0 or (g == 0 and t0 < 2):
                     nc.sync.dma_start(rows[:, t0 : t0 + per_bank, :], dst)
@@ -344,54 +337,50 @@ def tile_list_face_transmissibility_kernel(
                 final = (i, g, c0 + unit) == (last, GROUPS - 1, w)
                 weave = nc.scalar.copy if final else nc.vector.tensor_copy
                 weave(
-                    y_bf[:, c0 * PACK : (c0 + unit) * PACK].rearrange("p (c i t) -> p c t i", i=4, t=PACK),
-                    y_tiles[i, g][:, :, c0 : c0 + unit].rearrange("p t (c i) -> p c t i", i=4),
+                    y_bf[:, c0 * PACK : (c0 + unit) * PACK].rearrange("p (c i t) -> p c t i", i=LINE, t=PACK),
+                    y_tiles[i, g][:, :, c0 : c0 + unit].rearrange("p t (c i) -> p c t i", i=LINE),
                 )
             for c0, unit in units:
                 cols = slice(j0 + c0, j0 + c0 + unit)
                 nc.vector.quantize_mx(
                     y_w[:, g, cols].bitcast(FP8X4), y_sc[:, g, cols], y_bf[:, c0 * PACK : (c0 + unit) * PACK]
                 )
-                if (i, g) == (last, 1):
-                    first = 0 if c0 == 0 else cols.start
+                if (i, g) == (last, GROUPS - 1):
+                    first = cols.start if c0 else 0
                     nc.sync.dma_start(out_words[:, g, first : cols.stop], y_w[:, g, first : cols.stop])
             if (i, g) == (last, 0):
                 nc.sync.dma_start(out_words[:, g, :], y_w[:, g, :])
 
-        make_roots(0, 128)
+        make_roots(0, P)
         square(0)
         quantise(0)
-        make_roots(128, 128)
-        make_roots(256, 128)
-        make_roots(384, 128)
-        square(128)
-        square(256)
-        square(384)
+        second = range(starts[1], starts[2], P)
+        for j in second:
+            make_roots(j, P)
+        for j in second:
+            square(j)
         make_y(0, 0)
-        quantise(128)
-        quantise(256)
-        quantise(384)
+        for j in second:
+            quantise(j)
         make_y(0, 1)
-        make_roots(512, 256)
-        make_roots(768, 256)
+        for j in range(starts[2], S, HALF):
+            make_roots(j, HALF)
         make_y(1, 0)
-        square(512)
-        square(640)
-        quantise(512)
-        square(768)
-        quantise(640)
-        square(896)
-        quantise(768)
-        quantise(896)
+        third = list(range(starts[2], S, P))
+        square(third[0])
+        for before, j in zip(third, third[1:]):
+            square(j)
+            quantise(before)
+        quantise(third[-1])
         make_y(1, 1)
-        make_y(2, 0)
-        make_y(2, 1)
+        for g in range(GROUPS):
+            make_y(last, g)
         for i in range(len(PIECES)):
             for g in range(GROUPS):
                 make_planes(i, g)
 
-        for q in range(4):
+        for q in range(QUADS):
             nc.scalar.dma_start(
-                out_2[:, 4 * q : 4 * q + 4, :].bitcast(I32).rearrange("g r n -> r g n"),
-                y_sc[32 * q : 32 * q + 4, :, :].bitcast(I32),
+                out_2[:, LIVE * q : LIVE * (q + 1), :].bitcast(I32).rearrange("g r n -> r g n"),
+                y_sc[live(q), :, :].bitcast(I32),
             )

@@ -27,6 +27,7 @@ BANK = 512
 CHUNK = 512
 CHUNKS = S // CHUNK
 HALF = CHUNK // 2
+MID = CHUNK - P
 LIST_ROWS = 16
 QUADS, QUAD, LIVE = 4, 32, 4
 SCALE_ROWS = QUADS * LIVE
@@ -38,6 +39,7 @@ TABLE_CUT = 1024
 PIECES = [128, 384, 512]
 VECTOR_BANKS = (0, 2, 3, 13)
 SCALAR_SQUARES = (384, 896)
+WO_ROW = 112
 PLANE_UNIT = 256
 
 
@@ -48,6 +50,7 @@ def tile_list_face_transmissibility_kernel(
     with ExitStack() as ctx:
         keep = ctx.enter_context(tc.tile_pool(name="keep", bufs=1))
         psum = ctx.enter_context(tc.psum_pool(name="psum", bufs=1))
+        chain = ctx.enter_context(tc.tile_pool(name="chain", bufs=1))
 
         def sb(shape, dtype, name, tag="", align=64):
             return keep.tile(shape, dtype, name=name, tag=tag or name, align_bytes=align)
@@ -62,16 +65,17 @@ def tile_list_face_transmissibility_kernel(
         nc.sync.dma_start(offsets[:], offs)
 
         tab_sc = sb([P, T], U8, "tab_sc", align=ROW_ALIGN)
-        wr_sc_raw = sb([P, PASSES * H], U8, "wr_sc_raw", "reused")
-        nc.vector.memset(wr_sc_raw[:].bitcast(I32), 0)
+        w_sc_raw = sb([P, PASSES * H], U8, "w_sc_raw", "reused")
+        for p0, p1 in ((0, 3 * QUAD), (3 * QUAD, WO_ROW)):
+            nc.vector.memset(w_sc_raw[p0:p1, :].bitcast(I32), 0)
         for p0, p1 in ((0, SCALE_ROW[0]), (QUAD, P // 2)):
             nc.vector.memset(tab_sc[p0:p1, :].bitcast(I32), 0)
             nc.gpsimd.memset(tab_sc[P // 2 + p0 : P // 2 + p1, :].bitcast(I32), 0)
         v_sc = [sb([P, S], U8, "v_sc%d" % a) for a in range(PASSES)]
         for a in range(PASSES):
             nc.vector.memset(v_sc[a][:].bitcast(I32), 0)
-        wo_sc_raw = sb([P, N], U8, "wo_sc_raw")
-        nc.vector.memset(wo_sc_raw[:].bitcast(I32), 0)
+        wo_sc = sb([P, N], U8, "wo_sc")
+        nc.vector.memset(wo_sc[:].bitcast(I32), 0)
 
         tab_w = [sb([P, T], I32, "tab_w%d" % a, align=ROW_ALIGN) for a in range(PASSES)]
 
@@ -84,10 +88,11 @@ def tile_list_face_transmissibility_kernel(
             queue.dma_start(
                 tab_sc[SCALE_ROW[a] : SCALE_ROW[a] + SCALE_ROWS, :].bitcast(I32), tab_scales[a].bitcast(I32)
             )
+        nc.scalar.dma_start(w_sc_raw[WO_ROW:, :].bitcast(I32), wo_scales[0].bitcast(I32))
         load_table(0, 0, TABLE_HEAD)
         for q in range(QUADS):
             nc.sync.dma_start(
-                wr_sc_raw[live(q), :].bitcast(I32).rearrange("r (a n) -> r a n", a=PASSES),
+                w_sc_raw[live(q), :].bitcast(I32).rearrange("r (a n) -> r a n", a=PASSES),
                 wr_scales[:, LIVE * q : LIVE * (q + 1), :].bitcast(I32).rearrange("a r n -> r a n"),
             )
         wr_raw = sb([P, PASSES * 2 * H], U8, "wr_raw")
@@ -107,19 +112,16 @@ def tile_list_face_transmissibility_kernel(
             if a == 0:
                 load_table(1, TABLE_CUT, T)
 
-        wl_parts = [(0, 0, PACK), (1, 0, PACK // 2), (1, PACK // 2, PACK)]
         wl_raw = []
-        for a, r0, r1 in wl_parts:
-            wl_raw.append(sb([P, r1 - r0, H], F32, "wl_raw%d_%d" % (a, r0), align=ROW_ALIGN))
-            nc.sync.dma_start(
-                wl_raw[-1][:], wl[a * KP : (a + 1) * KP, :].rearrange("(p r) c -> p r c", r=PACK)[:, r0:r1, :]
-            )
+        for a in range(PASSES):
+            wl_raw.append(sb([P, PACK, H], F32, "wl_raw%d" % a, align=ROW_ALIGN))
+            rows = wl[a * KP : (a + 1) * KP, :].rearrange("(p r) c -> p r c", r=PACK)
+            for r0, r1 in ((0, 2), (2, PACK)) if a else ((0, PACK),):
+                nc.sync.dma_start(wl_raw[a][:, r0:r1, :], rows[:, r0:r1, :])
         mob_sb = sb([P, PACK], F32, "mob_sb")
         nc.sync.dma_start(mob_sb[:], mob.rearrange("(p t) -> p t", t=PACK))
-        for q in range(QUADS):
-            nc.sync.dma_start(
-                wo_sc_raw[live(q), :].bitcast(I32), wo_scales[0, LIVE * q : LIVE * (q + 1), :].bitcast(I32)
-            )
+        wo_raw = sb([P, N], I32, "wo_raw", align=ROW_ALIGN)
+        nc.sync.dma_start(wo_raw[:], wo_words[0].rearrange("p n t -> p (n t)").bitcast(I32))
 
         wr_w = sb([P, PASSES * 2 * H], U8, "wr_w")
         nc.vector.tensor_copy(
@@ -129,8 +131,11 @@ def tile_list_face_transmissibility_kernel(
         wr_sc = sb([P, PASSES * H], U8, "wr_sc")
         nc.vector.tensor_copy(
             wr_sc[:].rearrange("p (a t m) -> p a m t", a=PASSES, t=PACK),
-            wr_sc_raw[:].rearrange("p (a m t) -> p a m t", a=PASSES, t=PACK),
+            w_sc_raw[:].rearrange("p (a m t) -> p a m t", a=PASSES, t=PACK),
         )
+        for q in range(QUADS):
+            row = WO_ROW + LIVE * q
+            nc.sync.dma_start(wo_sc[live(q), :].bitcast(I32), wr_sc[row : row + LIVE, :].bitcast(I32))
 
         v_w = {}
         for a in range(PASSES):
@@ -148,21 +153,20 @@ def tile_list_face_transmissibility_kernel(
             c, c0 = divmod(j0, CHUNK)
             return v_w[a, c][:, c0 : c0 + w].bitcast(FP8X4), v_sc[a][:, j0 : j0 + w]
 
-        def first_stage(weight, name, order):
-            res = [sb([P, PACK, CHUNK], F32, "%s%d" % (name, c)) for c in range(CHUNKS)]
+        def first_stage(weight, order):
             acc = {}
             for a in range(PASSES):
-                for b, sums in order:
+                for b, sums, dst in order:
                     if a == 0:
                         acc[b] = bank(b)
-                    w = BANK // len(sums)
-                    for e, (r0, j0) in enumerate(sums):
-                        if j0 < CHUNK:
+                    c0 = 0
+                    for e, (r0, j0, w) in enumerate(sums):
+                        if P <= j0 < CHUNK:
                             lhs, rhs = weight(a, r0, P), table(a, j0, w)
                         else:
                             lhs, rhs = table(a, j0, P), weight(a, r0, w)
                         nc.tensor.matmul_mx(
-                            acc[b][:, e * w : (e + 1) * w],
+                            acc[b][:, c0 : c0 + w],
                             lhsT=lhs[0],
                             lhsT_scale=lhs[1],
                             rhs=rhs[0],
@@ -170,95 +174,113 @@ def tile_list_face_transmissibility_kernel(
                             start=(a == 0 and e == 0),
                             stop=(a == PASSES - 1 and e == len(sums) - 1),
                         )
-            for b, sums in order:
-                r0, j0 = sums[0]
-                w = BANK // len(sums)
-                if j0 < CHUNK:
-                    dst = res[0][:, r0 // P : r0 // P + len(sums), j0 : j0 + w]
-                else:
-                    block = (j0 - CHUNK) // P
-                    dst = res[1][:, block : block + len(sums), r0 : r0 + w]
-                nc.scalar.activation(dst, acc[b][:].rearrange("p (e j) -> p e j", e=len(sums)), ACT.Exp)
-            return res
+                        c0 = c0 + w
+            for b, sums, dst in order:
+                nc.scalar.activation(dst, acc[b][:].rearrange("p (e j) -> p e j", e=dst.shape[1]), ACT.Exp)
 
         def wr_columns(a, r0, w):
             c0 = a * H + r0
             return wr_w[:, 2 * c0 : 2 * (c0 + w)].bitcast(FP4X4), wr_sc[:, c0 : c0 + w]
 
-        rr_order = [
-            (2 * quarter + pair, [((2 * pair + e) * P, quarter * HALF) for e in range(2)])
-            for quarter in range(2)
-            for pair in range(2)
-        ]
-        rr_order.extend([(PACK + block, [(0, CHUNK + block * P)]) for block in range(PACK)])
-        rr = first_stage(wr_columns, "rr", rr_order)
+        rr_early = sb([P, 1, H], F32, "rr_early")
+        rr_mid = sb([P, PACK, MID], F32, "rr_mid")
+        rr_late = sb([P, PACK, H], F32, "rr_late")
+        rr_order = [(0, [(0, 0, H)], rr_early[:]), (1, [(t * P, P, P) for t in range(PACK)], rr_mid[:, :, :P])]
+        for pair in range(2):
+            sums = [((2 * pair + e) * P, HALF, HALF) for e in range(2)]
+            rr_order.append((2 + pair, sums, rr_mid[:, 2 * pair : 2 * pair + 2, P:]))
+        for block in range(PACK):
+            rr_order.append((PACK + block, [(0, CHUNK + block * P, H)], rr_late[:, block : block + 1, :]))
+        first_stage(wr_columns, rr_order)
 
-        wl_w = [sb([P, H], U32, "wl_w%d" % a) for a in range(PASSES)]
-        wl_sc = [sb([P, H], U8, "wl_sc%d" % a) for a in range(PASSES)]
+        wl_w = [sb([P, PASSES, HALF], U32, "wl_w%d" % pair) for pair in range(2)]
+        wl_sc = [sb([P, PASSES, HALF], U8, "wl_sc%d" % pair) for pair in range(2)]
 
-        def quantise_wl(a, t0, span, tag):
-            rounded = sb([P, span * KP], BF16, "wl_bf%d%d" % (a, t0), tag)
-            for raw, (part_pass, r0, r1) in zip(wl_raw, wl_parts):
-                if part_pass == a:
-                    nc.vector.tensor_copy(
-                        rounded[:].rearrange("p (t m r) -> p m r t", t=span, r=PACK)[:, :, r0:r1, :],
-                        raw[:].rearrange("p r (m t) -> p m r t", t=PACK)[:, :, :, t0 : t0 + span],
-                    )
-            cols = slice(t0 * P, (t0 + span) * P)
-            nc.vector.quantize_mx(wl_w[a][:, cols].bitcast(FP8X4), wl_sc[a][:, cols], rounded[:])
+        def round_wl(a, pair, rounded, r0=0, r1=PACK, m0=0, m1=P):
+            nc.vector.tensor_copy(
+                rounded.rearrange("p (t m r) -> p m r t", t=2, r=PACK)[:, m0:m1, r0:r1, :],
+                wl_raw[a][:, r0:r1, :].rearrange("p r (m t) -> p m r t", t=PACK)[:, m0:m1, :, 2 * pair : 2 * pair + 2],
+            )
 
-        quantise_wl(0, 0, 2, "")
-        for t in range(2):
-            quantise_wl(1, t, 1, "wl_held%d" % t)
-        for a in range(PASSES):
-            quantise_wl(a, 2, 2, "wl_held%d" % a)
+        first_bf = sb([P, 2 * KP], BF16, "first_bf")
+        round_wl(0, 0, first_bf[:])
+        nc.vector.quantize_mx(wl_w[0][:, 0, :].bitcast(FP8X4), wl_sc[0][:, 0, :], first_bf[:])
+        wl_bf = chain.tile([P, PASSES * 2 * KP], BF16, name="wl_bf", offset=3072, align_bytes=64)
+        middle = wl_bf[:, 3 * HALF : 3 * HALF + 2 * KP]
+        round_wl(1, 0, middle, 0, 2)
+        round_wl(0, 1, wl_bf[:, : 2 * KP], m1=P // 2)
+        round_wl(1, 0, middle, 2, PACK)
+        for e in range(2):
+            cols = slice(e * P, (e + 1) * P)
+            nc.vector.quantize_mx(
+                wl_w[0][:, 1, cols].bitcast(FP8X4), wl_sc[0][:, 1, cols], middle[:, e * KP : (e + 1) * KP]
+            )
+        round_wl(0, 1, wl_bf[:, : 2 * KP], m0=P // 2)
+        round_wl(1, 1, wl_bf[:, 2 * KP :])
+        nc.vector.quantize_mx(
+            wl_w[1][:].rearrange("p a c -> p (a c)").bitcast(FP8X4),
+            wl_sc[1][:].rearrange("p a c -> p (a c)"),
+            wl_bf[:],
+        )
+
 
         def wl_columns(a, r0, w):
-            return wl_w[a][:, r0 : r0 + w].bitcast(FP8X4), wl_sc[a][:, r0 : r0 + w]
+            pair, c0 = divmod(r0, HALF)
+            return wl_w[pair][:, a, c0 : c0 + w].bitcast(FP8X4), wl_sc[pair][:, a, c0 : c0 + w]
 
-        rl_order = []
-        for pair in range(2):
-            rl_order.extend([(PACK * pair + e, [((2 * pair + e) * P, 0)]) for e in range(2)])
-            rl_order.extend(
-                [
-                    (PACK * pair + 2 + two, [(pair * HALF, CHUNK + (2 * two + e) * P) for e in range(2)])
-                    for two in range(2)
-                ]
-            )
-        rl = first_stage(wl_columns, "rl", rl_order)
-
-        inv_mob = sb([P, PACK], F32, "inv_mob", "wl_sc1")
-        nc.vector.reciprocal(inv_mob[:], mob_sb[:])
-
-        total = [[], []]
-        for t in range(PACK):
-            total[0].append(sb([P, CHUNK], F32, "total%d" % t, "" if t else "wl_held1"))
-            nc.vector.tensor_tensor(total[0][t][:], rl[0][:, t, :], rr[0][:, t, :], ALU.add)
-        for t in range(PACK):
-            total[1].append(bank(PACK + t))
-            for term in (rr, rl):
-                for block in range(PACK):
+        def add_turned(out, terms):
+            depth = len(terms[0])
+            for d in range(depth):
+                for i, term in enumerate(terms):
                     nc.tensor.matmul(
-                        total[1][t][:, block * P : (block + 1) * P],
-                        lhsT=term[1][:, block, t * P : (t + 1) * P],
+                        out[:, i * P : (i + 1) * P],
+                        lhsT=term[d],
                         rhs=ident[:],
                         is_transpose=True,
-                        start=(term is rr and block == 0),
-                        stop=(term is rl and block == PACK - 1),
+                        start=(d == 0 and i == 0),
+                        stop=(d == depth - 1 and i == len(terms) - 1),
                     )
 
-        wo_raw = sb([P, N], I32, "wo_raw", "wl_raw1_2", align=ROW_ALIGN)
-        nc.sync.dma_start(wo_raw[:], wo_words[0].rearrange("p n t -> p (n t)").bitcast(I32))
-        wo_w = sb([P, N], I32, "wo_w")
-        nc.vector.tensor_copy(
-            wo_w[:].rearrange("p (g t m) -> p g m t", g=GROUPS, t=PACK),
-            wo_raw[:].rearrange("p (g m t) -> p g m t", g=GROUPS, t=PACK),
+        behind_wl = chain.tile([P, BANK + 2 * MID], F32, name="behind_wl", offset=0, align_bytes=64)
+        inverse = behind_wl[:, :BANK]
+        later_sums = sb([P, 2 * MID], F32, "later_sums")
+        totals = [behind_wl[:, BANK : BANK + MID], behind_wl[:, BANK + MID :], later_sums[:, :MID], later_sums[:, MID:]]
+        rl_first = sb([P, PACK, BANK], F32, "rl_first")
+        rl_late = sb([P, PACK, H], F32, "rl_late")
+        for pair in range(2):
+            order = []
+            for t in (2 * pair, 2 * pair + 1):
+                sums = [(t * P, P, P), (t * P, HALF, HALF), (t * P, 0, P)]
+                order.append((t % 2, sums, rl_first[:, t : t + 1, :]))
+            for two in range(2):
+                sums = [(pair * HALF, CHUNK + (2 * two + e) * P, HALF) for e in range(2)]
+                order.append((2 + two, sums, rl_late[:, 2 * two : 2 * two + 2, pair * HALF : (pair + 1) * HALF]))
+            for part in [[unit] for unit in order] if pair else [order]:
+                first_stage(wl_columns, part)
+            if pair:
+                inv_mob = sb([P, PACK], F32, "inv_mob", "wl_sc1")
+                nc.vector.reciprocal(inv_mob[:], mob_sb[:])
+            for t in (2 * pair, 2 * pair + 1):
+                early = bank((6, 5, 0, 1)[t])
+                add_turned(early, [(rl_first[:, t, MID:], rr_early[:, 0, t * P : (t + 1) * P])])
+                nc.vector.reciprocal(inverse[:, t * P : (t + 1) * P], early[:, :P])
+                nc.gpsimd.tensor_tensor(totals[t], rl_first[:, t, :MID], rr_mid[:, t, :], ALU.add)
+        wo_w = chain.tile([P, N], I32, name="wo_w", offset=5120, align_bytes=64)
+        nc.gpsimd.tensor_copy(
+            wo_w[:].rearrange("p (g t m) -> p g t m", g=GROUPS, t=PACK),
+            wo_raw[:].rearrange("p (g m t) -> p g t m", g=GROUPS, t=PACK),
         )
-        wo_sc = sb([P, N], U8, "wo_sc", "wl_raw1_2", align=ROW_ALIGN)
-        nc.vector.tensor_copy(
-            wo_sc[:].rearrange("p (g t m) -> p g m t", g=GROUPS, t=PACK),
-            wo_sc_raw[:].rearrange("p (g m t) -> p g m t", g=GROUPS, t=PACK),
-        )
+
+        late = []
+        for t in range(PACK):
+            late.append(bank(PACK + t))
+            cols = slice(t * P, (t + 1) * P)
+            add_turned(late[t], [(rl_late[:, block, cols], rr_late[:, block, cols]) for block in range(PACK)])
+
+        def total(t, j0, w):
+            if j0 >= CHUNK:
+                return late[t][:, j0 - CHUNK : j0 - CHUNK + w]
+            return totals[t][:, j0 - P : j0 - P + w]
 
         y_sc = sb([P, GROUPS, S], U8, "y_sc")
         y_w = sb([P, GROUPS, S], I32, "y_w", align=ROW_ALIGN)
@@ -277,11 +299,10 @@ def tile_list_face_transmissibility_kernel(
         h_bf = {}
 
         def make_roots(j0, w):
-            c, c0 = divmod(j0, CHUNK)
-            root = sb([P, PACK, w], F32, "root%d" % j0)
+            root = sb([P, PACK, w], F32, "root%d" % j0, "")
             for t in range(PACK):
                 nc.scalar.activation(
-                    root[:, t, :], total[c][t][:, c0 : c0 + w], ACT.Abs_reciprocal_sqrt, scale=inv_mob[:, t : t + 1]
+                    root[:, t, :], total(t, j0, w), ACT.Abs_reciprocal_sqrt, scale=inv_mob[:, t : t + 1]
                 )
             for u0 in range(0, w, P):
                 roots[j0 + u0] = root[:, :, u0 : u0 + P]
@@ -307,7 +328,7 @@ def tile_list_face_transmissibility_kernel(
             rows = out_0[g * KP : (g + 1) * KP, j0 : j0 + w].rearrange("(p t) j -> p t j", t=PACK)
             spans = [(0, P), (P, 2 * P)] if w == 3 * P else [(0, w)]
             for t0 in range(0, PACK, per_bank):
-                acc = bank(PACK * (1 - g) + t0 if i == last else len(used) % PACK)
+                acc = bank(((4, 5, 6, 7) if (i, g) == (last, 0) else (2, 3, 0, 1))[(len(used) - (2 if i == last else 0)) % PACK])
                 for e in range(per_bank):
                     s0 = (g * PACK + t0 + e) * P
                     for c0, n in spans:
@@ -351,8 +372,13 @@ def tile_list_face_transmissibility_kernel(
             if (i, g) == (last, 0):
                 nc.sync.dma_start(out_words[:, g, :], y_w[:, g, :])
 
-        make_roots(0, P)
-        square(0)
+        h_bf[0] = sb([P, P * PACK], BF16, "h_bf0")
+        nc.vector.tensor_tensor(
+            h_bf[0][:].rearrange("p (c i t) -> p c t i", i=LINE, t=PACK),
+            inverse.rearrange("p (t c i) -> p c t i", i=LINE, t=PACK),
+            mob_sb[:].unsqueeze(1).unsqueeze(3).to_broadcast([P, P // LINE, PACK, LINE]),
+            ALU.mult,
+        )
         quantise(0)
         second = range(starts[1], starts[2], P)
         for j in second:

@@ -50,7 +50,6 @@ def tile_list_face_transmissibility_kernel(
     with ExitStack() as ctx:
         keep = ctx.enter_context(tc.tile_pool(name="keep", bufs=1))
         psum = ctx.enter_context(tc.psum_pool(name="psum", bufs=1))
-        chain = ctx.enter_context(tc.tile_pool(name="chain", bufs=1))
 
         def sb(shape, dtype, name, tag="", align=64):
             return keep.tile(shape, dtype, name=name, tag=tag or name, align_bytes=align)
@@ -205,7 +204,7 @@ def tile_list_face_transmissibility_kernel(
         first_bf = sb([P, 2 * KP], BF16, "first_bf")
         round_wl(0, 0, first_bf[:])
         nc.vector.quantize_mx(wl_w[0][:, 0, :].bitcast(FP8X4), wl_sc[0][:, 0, :], first_bf[:])
-        wl_bf = chain.tile([P, PASSES * 2 * KP], BF16, name="wl_bf", offset=3072, align_bytes=64)
+        wl_bf = sb([P, PASSES * 2 * KP], BF16, "wl_bf")
         middle = wl_bf[:, 3 * HALF : 3 * HALF + 2 * KP]
         round_wl(1, 0, middle, 0, 2)
         round_wl(0, 1, wl_bf[:, : 2 * KP], m1=P // 2)
@@ -224,6 +223,12 @@ def tile_list_face_transmissibility_kernel(
         )
 
 
+        wo_w = sb([P, N], I32, "wo_w", "wl_bf")
+        nc.vector.tensor_copy(
+            wo_w[:].rearrange("p (g t m) -> p g m t", g=GROUPS, t=PACK),
+            wo_raw[:].rearrange("p (g m t) -> p g m t", g=GROUPS, t=PACK),
+        )
+
         def wl_columns(a, r0, w):
             pair, c0 = divmod(r0, HALF)
             return wl_w[pair][:, a, c0 : c0 + w].bitcast(FP8X4), wl_sc[pair][:, a, c0 : c0 + w]
@@ -241,7 +246,7 @@ def tile_list_face_transmissibility_kernel(
                         stop=(d == depth - 1 and i == len(terms) - 1),
                     )
 
-        behind_wl = chain.tile([P, BANK + 2 * MID], F32, name="behind_wl", offset=0, align_bytes=64)
+        behind_wl = sb([P, BANK + 2 * MID], F32, "behind_wo", "wo_raw", align=ROW_ALIGN)
         inverse = behind_wl[:, :BANK]
         later_sums = sb([P, 2 * MID], F32, "later_sums")
         totals = [behind_wl[:, BANK : BANK + MID], behind_wl[:, BANK + MID :], later_sums[:, :MID], later_sums[:, MID:]]
@@ -251,25 +256,20 @@ def tile_list_face_transmissibility_kernel(
             order = []
             for t in (2 * pair, 2 * pair + 1):
                 sums = [(t * P, P, P), (t * P, HALF, HALF), (t * P, 0, P)]
-                order.append((t % 2, sums, rl_first[:, t : t + 1, :]))
+                order.append((PACK * pair + t % 2, sums, rl_first[:, t : t + 1, :]))
             for two in range(2):
                 sums = [(pair * HALF, CHUNK + (2 * two + e) * P, HALF) for e in range(2)]
-                order.append((2 + two, sums, rl_late[:, 2 * two : 2 * two + 2, pair * HALF : (pair + 1) * HALF]))
+                order.append((PACK * pair + 2 + two, sums, rl_late[:, 2 * two : 2 * two + 2, pair * HALF : (pair + 1) * HALF]))
             for part in [[unit] for unit in order] if pair else [order]:
                 first_stage(wl_columns, part)
             if pair:
                 inv_mob = sb([P, PACK], F32, "inv_mob", "wl_sc1")
                 nc.vector.reciprocal(inv_mob[:], mob_sb[:])
             for t in (2 * pair, 2 * pair + 1):
-                early = bank((6, 5, 0, 1)[t])
+                early = bank(t)
                 add_turned(early, [(rl_first[:, t, MID:], rr_early[:, 0, t * P : (t + 1) * P])])
                 nc.vector.reciprocal(inverse[:, t * P : (t + 1) * P], early[:, :P])
                 nc.gpsimd.tensor_tensor(totals[t], rl_first[:, t, :MID], rr_mid[:, t, :], ALU.add)
-        wo_w = chain.tile([P, N], I32, name="wo_w", offset=5120, align_bytes=64)
-        nc.gpsimd.tensor_copy(
-            wo_w[:].rearrange("p (g t m) -> p g t m", g=GROUPS, t=PACK),
-            wo_raw[:].rearrange("p (g m t) -> p g t m", g=GROUPS, t=PACK),
-        )
 
         late = []
         for t in range(PACK):
@@ -328,7 +328,7 @@ def tile_list_face_transmissibility_kernel(
             rows = out_0[g * KP : (g + 1) * KP, j0 : j0 + w].rearrange("(p t) j -> p t j", t=PACK)
             spans = [(0, P), (P, 2 * P)] if w == 3 * P else [(0, w)]
             for t0 in range(0, PACK, per_bank):
-                acc = bank(((4, 5, 6, 7) if (i, g) == (last, 0) else (2, 3, 0, 1))[(len(used) - (2 if i == last else 0)) % PACK])
+                acc = bank(((4, 5, 6, 7) if (i, g) == (last, 0) else (0, 1, 2, 3))[(len(used) - (2 if i == last else 0)) % PACK])
                 for e in range(per_bank):
                     s0 = (g * PACK + t0 + e) * P
                     for c0, n in spans:

from contextlib import ExitStack

import concourse.mybir as mybir
from concourse.masks import make_identity

K, T, S, H, N = 1024, 4096, 1024, 512, 1024
FLOPS = 2 * K * H * S * 2 + 2 * H * N * S

F32 = mybir.dt.float32
BF16 = mybir.dt.bfloat16
I32 = mybir.dt.int32
U32 = mybir.dt.uint32
U16 = mybir.dt.uint16
U8 = mybir.dt.uint8
FP8X4 = mybir.dt.float8_e4m3fn_x4
FP4X4 = mybir.dt.float4_e2m1fn_x4
ACT = mybir.ActivationFunctionType
ALU = mybir.AluOpType

P = 128
PACK = 4
KP = P * PACK
PASSES = K // KP
GROUPS = N // KP
BANKS = 8
BANK = 512
CHUNK = 512
CHUNKS = S // CHUNK
HALF = CHUNK // 2
MID = CHUNK - P
LIST_ROWS = 16
QUADS, QUAD, LIVE = 4, 32, 4
SCALE_ROWS = QUADS * LIVE
LINE = 4
ROW_ALIGN = 256
SCALE_ROW = (16, 80)
TABLE_HEAD = 3072
TABLE_CUT = 1024
PIECES = [128, 384, 512]
VECTOR_BANKS = (0, 2, 3, 13)
SCALAR_SQUARES = (384, 896)
WO_ROW = 112
PLANE_UNIT = 256


def tile_list_face_transmissibility_kernel(
    tc, tab_words, tab_scales, offs, wl, wr_words, wr_scales, mob, wo_words, wo_scales, out_0, out_1, out_2
):
    nc = tc.nc
    with ExitStack() as ctx:
        keep = ctx.enter_context(tc.tile_pool(name="keep", bufs=1))
        psum = ctx.enter_context(tc.psum_pool(name="psum", bufs=1))

        def sb(shape, dtype, name, tag="", align=64):
            return keep.tile(shape, dtype, name=name, tag=tag or name, align_bytes=align)

        def bank(b):
            return psum.tile([P, BANK], F32, name="bank%d" % (b % BANKS))

        def live(q):
            return slice(QUAD * q, QUAD * q + LIVE)

        offsets = keep.tile([P, S // LIST_ROWS], U16, name="offsets")
        nc.sync.dma_start(offsets[:], offs)

        tab_sc = sb([P, T], U8, "tab_sc", align=ROW_ALIGN)
        w_sc_raw = sb([P, PASSES * H], U8, "w_sc_raw", "reused")
        for p0, p1 in ((0, 3 * QUAD), (3 * QUAD, WO_ROW)):
            nc.vector.memset(w_sc_raw[p0:p1, :].bitcast(I32), 0)
        for p0, p1 in ((0, SCALE_ROW[0]), (QUAD, P // 2)):
            nc.vector.memset(tab_sc[p0:p1, :].bitcast(I32), 0)
            nc.gpsimd.memset(tab_sc[P // 2 + p0 : P // 2 + p1, :].bitcast(I32), 0)
        v_sc = [sb([P, S], U8, "v_sc%d" % a) for a in range(PASSES)]
        for a in range(PASSES):
            nc.vector.memset(v_sc[a][:].bitcast(I32), 0)
        wo_sc = sb([P, N], U8, "wo_sc")
        nc.vector.memset(wo_sc[:].bitcast(I32), 0)

        tab_w = [sb([P, T], I32, "tab_w%d" % a, align=ROW_ALIGN) for a in range(PASSES)]

        def load_table(a, c0, c1):
            nc.sync.dma_start(
                tab_w[a][:, c0:c1], tab_words[a].rearrange("p n t -> p (n t)").bitcast(I32)[:, c0:c1]
            )

        for a, queue in enumerate((nc.sync, nc.scalar)):
            queue.dma_start(
                tab_sc[SCALE_ROW[a] : SCALE_ROW[a] + SCALE_ROWS, :].bitcast(I32), tab_scales[a].bitcast(I32)
            )
        nc.scalar.dma_start(w_sc_raw[WO_ROW:, :].bitcast(I32), wo_scales[0].bitcast(I32))
        load_table(0, 0, TABLE_HEAD)
        for q in range(QUADS):
            nc.sync.dma_start(
                w_sc_raw[live(q), :].bitcast(I32).rearrange("r (a n) -> r a n", a=PASSES),
                wr_scales[:, LIVE * q : LIVE * (q + 1), :].bitcast(I32).rearrange("a r n -> r a n"),
            )
        wr_raw = sb([P, PASSES * 2 * H], U8, "wr_raw")
        nc.sync.dma_start(
            wr_raw[:].bitcast(I32).rearrange("p (a n) -> p a n", a=PASSES),
            wr_words.bitcast(I32).rearrange("a p n -> p a n"),
        )
        load_table(0, TABLE_HEAD, T)
        load_table(1, 0, TABLE_CUT)

        picked_sc = sb([P, S], U8, "picked_sc")
        nc.vector.tensor_copy(picked_sc[:], tab_sc[:].indirect(offsets[:]))
        for a in range(PASSES):
            for q in range(QUADS):
                row = SCALE_ROW[a] + LIVE * q
                nc.sync.dma_start(v_sc[a][live(q), :].bitcast(I32), picked_sc[row : row + LIVE, :].bitcast(I32))
            if a == 0:
                load_table(1, TABLE_CUT, T)

        wl_raw = []
        for a in range(PASSES):
            wl_raw.append(sb([P, PACK, H], F32, "wl_raw%d" % a, align=ROW_ALIGN))
            rows = wl[a * KP : (a + 1) * KP, :].rearrange("(p r) c -> p r c", r=PACK)
            for r0, r1 in ((0, 2), (2, PACK)) if a else ((0, PACK),):
                nc.sync.dma_start(wl_raw[a][:, r0:r1, :], rows[:, r0:r1, :])
        mob_sb = sb([P, PACK], F32, "mob_sb")
        nc.sync.dma_start(mob_sb[:], mob.rearrange("(p t) -> p t", t=PACK))
        wo_raw = sb([P, N], I32, "wo_raw", align=ROW_ALIGN)
        nc.sync.dma_start(wo_raw[:], wo_words[0].rearrange("p n t -> p (n t)").bitcast(I32))

        wr_w = sb([P, PASSES * 2 * H], U8, "wr_w")
        nc.vector.tensor_copy(
            wr_w[:].bitcast(U16).rearrange("p (a t m) -> p a m t", a=PASSES, t=PACK),
            wr_raw[:].bitcast(U16).rearrange("p (a m t) -> p a m t", a=PASSES, t=PACK),
        )
        wr_sc = sb([P, PASSES * H], U8, "wr_sc")
        nc.vector.tensor_copy(
            wr_sc[:].rearrange("p (a t m) -> p a m t", a=PASSES, t=PACK),
            w_sc_raw[:].rearrange("p (a m t) -> p a m t", a=PASSES, t=PACK),
        )
        for q in range(QUADS):
            row = WO_ROW + LIVE * q
            nc.sync.dma_start(wo_sc[live(q), :].bitcast(I32), wr_sc[row : row + LIVE, :].bitcast(I32))

        v_w = {}
        for a in range(PASSES):
            for c in range(CHUNKS):
                v_w[a, c] = sb([P, CHUNK], U32, "v_w%d_%d" % (a, c), "reused" if (a, c) == (0, 1) else "")
                cuts = (0, HALF, CHUNK) if (a, c) == (PASSES - 1, 0) else (0, CHUNK)
                for j0, j1 in zip(cuts, cuts[1:]):
                    listed = offsets[:, (c * CHUNK + j0) // LIST_ROWS : (c * CHUNK + j1) // LIST_ROWS]
                    nc.vector.tensor_copy(v_w[a, c][:, j0:j1], tab_w[a][:].bitcast(U32).indirect(listed))

        ident = sb([P, P], F32, "ident")
        make_identity(nc, ident[:])

        def table(a, j0, w):
            c, c0 = divmod(j0, CHUNK)
            return v_w[a, c][:, c0 : c0 + w].bitcast(FP8X4), v_sc[a][:, j0 : j0 + w]

        def first_stage(weight, order):
            acc = {}
            for a in range(PASSES):
                for b, sums, dst in order:
                    if a == 0:
                        acc[b] = bank(b)
                    c0 = 0
                    for e, (r0, j0, w) in enumerate(sums):
                        if P <= j0 < CHUNK:
                            lhs, rhs = weight(a, r0, P), table(a, j0, w)
                        else:
                            lhs, rhs = table(a, j0, P), weight(a, r0, w)
                        nc.tensor.matmul_mx(
                            acc[b][:, c0 : c0 + w],
                            lhsT=lhs[0],
                            lhsT_scale=lhs[1],
                            rhs=rhs[0],
                            rhs_scale=rhs[1],
                            start=(a == 0 and e == 0),
                            stop=(a == PASSES - 1 and e == len(sums) - 1),
                        )
                        c0 = c0 + w
            for b, sums, dst in order:
                nc.scalar.activation(dst, acc[b][:].rearrange("p (e j) -> p e j", e=dst.shape[1]), ACT.Exp)

        def wr_columns(a, r0, w):
            c0 = a * H + r0
            return wr_w[:, 2 * c0 : 2 * (c0 + w)].bitcast(FP4X4), wr_sc[:, c0 : c0 + w]

        rr_early = sb([P, 1, H], F32, "rr_early")
        rr_mid = sb([P, PACK, MID], F32, "rr_mid")
        rr_late = sb([P, PACK, H], F32, "rr_late")
        rr_order = [(0, [(0, 0, H)], rr_early[:]), (1, [(t * P, P, P) for t in range(PACK)], rr_mid[:, :, :P])]
        for pair in range(2):
            sums = [((2 * pair + e) * P, HALF, HALF) for e in range(2)]
            rr_order.append((2 + pair, sums, rr_mid[:, 2 * pair : 2 * pair + 2, P:]))
        for block in range(PACK):
            rr_order.append((PACK + block, [(0, CHUNK + block * P, H)], rr_late[:, block : block + 1, :]))
        first_stage(wr_columns, rr_order)

        wl_w = [sb([P, PASSES, HALF], U32, "wl_w%d" % pair) for pair in range(2)]
        wl_sc = [sb([P, PASSES, HALF], U8, "wl_sc%d" % pair) for pair in range(2)]

        def round_wl(a, pair, rounded, r0=0, r1=PACK, m0=0, m1=P):
            nc.vector.tensor_copy(
                rounded.rearrange("p (t m r) -> p m r t", t=2, r=PACK)[:, m0:m1, r0:r1, :],
                wl_raw[a][:, r0:r1, :].rearrange("p r (m t) -> p m r t", t=PACK)[:, m0:m1, :, 2 * pair : 2 * pair + 2],
            )

        first_bf = sb([P, 2 * KP], BF16, "first_bf")
        round_wl(0, 0, first_bf[:])
        nc.vector.quantize_mx(wl_w[0][:, 0, :].bitcast(FP8X4), wl_sc[0][:, 0, :], first_bf[:])
        wl_bf = sb([P, PASSES * 2 * KP], BF16, "wl_bf")
        middle = wl_bf[:, 3 * HALF : 3 * HALF + 2 * KP]
        round_wl(1, 0, middle, 0, 2)
        round_wl(0, 1, wl_bf[:, : 2 * KP], m1=P // 2)
        round_wl(1, 0, middle, 2, PACK)
        for e in range(2):
            cols = slice(e * P, (e + 1) * P)
            nc.vector.quantize_mx(
                wl_w[0][:, 1, cols].bitcast(FP8X4), wl_sc[0][:, 1, cols], middle[:, e * KP : (e + 1) * KP]
            )
        round_wl(0, 1, wl_bf[:, : 2 * KP], m0=P // 2)
        round_wl(1, 1, wl_bf[:, 2 * KP :])
        nc.vector.quantize_mx(
            wl_w[1][:].rearrange("p a c -> p (a c)").bitcast(FP8X4),
            wl_sc[1][:].rearrange("p a c -> p (a c)"),
            wl_bf[:],
        )


        wo_w = sb([P, N], I32, "wo_w", "wl_bf")
        nc.vector.tensor_copy(
            wo_w[:].rearrange("p (g t m) -> p g m t", g=GROUPS, t=PACK),
            wo_raw[:].rearrange("p (g m t) -> p g m t", g=GROUPS, t=PACK),
        )

        def wl_columns(a, r0, w):
            pair, c0 = divmod(r0, HALF)
            return wl_w[pair][:, a, c0 : c0 + w].bitcast(FP8X4), wl_sc[pair][:, a, c0 : c0 + w]

        def add_turned(out, terms):
            depth = len(terms[0])
            for d in range(depth):
                for i, term in enumerate(terms):
                    nc.tensor.matmul(
                        out[:, i * P : (i + 1) * P],
                        lhsT=term[d],
                        rhs=ident[:],
                        is_transpose=True,
                        start=(d == 0 and i == 0),
                        stop=(d == depth - 1 and i == len(terms) - 1),
                    )

        behind_wl = sb([P, BANK + 2 * MID], F32, "behind_wo", "wo_raw", align=ROW_ALIGN)
        inverse = behind_wl[:, :BANK]
        later_sums = sb([P, 2 * MID], F32, "later_sums")
        totals = [behind_wl[:, BANK : BANK + MID], behind_wl[:, BANK + MID :], later_sums[:, :MID], later_sums[:, MID:]]
        rl_first = sb([P, PACK, BANK], F32, "rl_first")
        rl_late = sb([P, PACK, H], F32, "rl_late")
        for pair in range(2):
            order = []
            for t in (2 * pair, 2 * pair + 1):
                sums = [(t * P, P, P), (t * P, HALF, HALF), (t * P, 0, P)]
                order.append((PACK * pair + t % 2, sums, rl_first[:, t : t + 1, :]))
            for two in range(2):
                sums = [(pair * HALF, CHUNK + (2 * two + e) * P, HALF) for e in range(2)]
                order.append((PACK * pair + 2 + two, sums, rl_late[:, 2 * two : 2 * two + 2, pair * HALF : (pair + 1) * HALF]))
            for part in [[unit] for unit in order] if pair else [order]:
                first_stage(wl_columns, part)
            if pair:
                inv_mob = sb([P, PACK], F32, "inv_mob", "wl_sc1")
                nc.vector.reciprocal(inv_mob[:], mob_sb[:])
            for t in (2 * pair, 2 * pair + 1):
                early = bank(t)
                add_turned(early, [(rl_first[:, t, MID:], rr_early[:, 0, t * P : (t + 1) * P])])
                nc.vector.reciprocal(inverse[:, t * P : (t + 1) * P], early[:, :P])
                nc.gpsimd.tensor_tensor(totals[t], rl_first[:, t, :MID], rr_mid[:, t, :], ALU.add)

        late = []
        for t in range(PACK):
            late.append(bank(PACK + t))
            cols = slice(t * P, (t + 1) * P)
            add_turned(late[t], [(rl_late[:, block, cols], rr_late[:, block, cols]) for block in range(PACK)])

        def total(t, j0, w):
            if j0 >= CHUNK:
                return late[t][:, j0 - CHUNK : j0 - CHUNK + w]
            return totals[t][:, j0 - P : j0 - P + w]

        y_sc = sb([P, GROUPS, S], U8, "y_sc")
        y_w = sb([P, GROUPS, S], I32, "y_w", align=ROW_ALIGN)
        out_words = out_1.rearrange("g p n t -> p g (n t)").bitcast(I32)
        starts = [sum(PIECES[:i]) for i in range(len(PIECES))]
        h_w = [sb([P, w], U32, "h_w%d" % i) for i, w in enumerate(PIECES)]
        h_sc = [sb([P, w], U8, "h_sc%d" % i) for i, w in enumerate(PIECES)]
        y_tiles = {
            (i, g): sb([P, PACK, w], F32, "y%d_%d" % (i, g), align=ROW_ALIGN)
            for i, w in enumerate(PIECES)
            for g in range(GROUPS)
        }
        last = len(PIECES) - 1
        used = []
        roots = {}
        h_bf = {}

        def make_roots(j0, w):
            root = sb([P, PACK, w], F32, "root%d" % j0, "")
            for t in range(PACK):
                nc.scalar.activation(
                    root[:, t, :], total(t, j0, w), ACT.Abs_reciprocal_sqrt, scale=inv_mob[:, t : t + 1]
                )
            for u0 in range(0, w, P):
                roots[j0 + u0] = root[:, :, u0 : u0 + P]

        def square(j):
            h_bf[j] = sb([P, P * PACK], BF16, "h_bf%d" % j, "h_bf0" if j == P else "")
            by_line = roots[j].rearrange("p t (c i) -> p c t i", i=LINE)
            woven = h_bf[j][:].rearrange("p (c i t) -> p c t i", i=LINE, t=PACK)
            if j in SCALAR_SQUARES:
                nc.scalar.activation(woven, by_line, ACT.Square)
            else:
                nc.vector.tensor_tensor(woven, by_line, by_line, ALU.mult)

        def quantise(j):
            i = max(piece for piece, j0 in enumerate(starts) if j0 <= j)
            cols = slice(j - starts[i], j - starts[i] + P)
            nc.vector.quantize_mx(h_w[i][:, cols].bitcast(FP8X4), h_sc[i][:, cols], h_bf[j][:])

        def make_y(i, g):
            j0, w = starts[i], PIECES[i]
            per_bank = BANK // w
            y = y_tiles[i, g]
            rows = out_0[g * KP : (g + 1) * KP, j0 : j0 + w].rearrange("(p t) j -> p t j", t=PACK)
            spans = [(0, P), (P, 2 * P)] if w == 3 * P else [(0, w)]
            for t0 in range(0, PACK, per_bank):
                acc = bank(((4, 5, 6, 7) if (i, g) == (last, 0) else (0, 1, 2, 3))[(len(used) - (2 if i == last else 0)) % PACK])
                for e in range(per_bank):
                    s0 = (g * PACK + t0 + e) * P
                    for c0, n in spans:
                        nc.tensor.matmul_mx(
                            acc[:, e * w + c0 : e * w + c0 + n],
                            lhsT=wo_w[:, s0 : s0 + P].bitcast(FP8X4),
                            lhsT_scale=wo_sc[:, s0 : s0 + P],
                            rhs=h_w[i][:, c0 : c0 + n].bitcast(FP8X4),
                            rhs_scale=h_sc[i][:, c0 : c0 + n],
                            start=True,
                            stop=True,
                        )
                dst = y[:, t0 : t0 + per_bank, :]
                empty = nc.vector.tensor_copy if len(used) in VECTOR_BANKS else nc.scalar.copy
                empty(dst, acc[:, : per_bank * w].rearrange("p (e j) -> p e j", e=per_bank))
                used.append(i)
                if i == 0 or (g == 0 and t0 < 2):
                    nc.sync.dma_start(rows[:, t0 : t0 + per_bank, :], dst)
                elif t0 % 2:
                    nc.sync.dma_start(rows[:, t0 - 1 : t0 + 1, :], y[:, t0 - 1 : t0 + 1, :])

        def make_planes(i, g):
            j0, w = starts[i], PIECES[i]
            units = [(c0, min(PLANE_UNIT, w - c0)) for c0 in range(0, w, PLANE_UNIT)]
            y_bf = sb([P, w * PACK], BF16, "y_bf%d_%d" % (i, g))
            for c0, unit in units:
                final = (i, g, c0 + unit) == (last, GROUPS - 1, w)
                weave = nc.scalar.copy if final else nc.vector.tensor_copy
                weave(
                    y_bf[:, c0 * PACK : (c0 + unit) * PACK].rearrange("p (c i t) -> p c t i", i=LINE, t=PACK),
                    y_tiles[i, g][:, :, c0 : c0 + unit].rearrange("p t (c i) -> p c t i", i=LINE),
                )
            for c0, unit in units:
                cols = slice(j0 + c0, j0 + c0 + unit)
                nc.vector.quantize_mx(
                    y_w[:, g, cols].bitcast(FP8X4), y_sc[:, g, cols], y_bf[:, c0 * PACK : (c0 + unit) * PACK]
                )
                if (i, g) == (last, GROUPS - 1):
                    first = cols.start if c0 else 0
                    nc.sync.dma_start(out_words[:, g, first : cols.stop], y_w[:, g, first : cols.stop])
            if (i, g) == (last, 0):
                nc.sync.dma_start(out_words[:, g, :], y_w[:, g, :])

        h_bf[0] = sb([P, P * PACK], BF16, "h_bf0")
        nc.vector.tensor_tensor(
            h_bf[0][:].rearrange("p (c i t) -> p c t i", i=LINE, t=PACK),
            inverse.rearrange("p (t c i) -> p c t i", i=LINE, t=PACK),
            mob_sb[:].unsqueeze(1).unsqueeze(3).to_broadcast([P, P // LINE, PACK, LINE]),
            ALU.mult,
        )
        quantise(0)
        second = range(starts[1], starts[2], P)
        for j in second:
            make_roots(j, P)
        for j in second:
            square(j)
        make_y(0, 0)
        for j in second:
            quantise(j)
        make_y(0, 1)
        for j in range(starts[2], S, HALF):
            make_roots(j, HALF)
        make_y(1, 0)
        third = list(range(starts[2], S, P))
        square(third[0])
        for before, j in zip(third, third[1:]):
            square(j)
            quantise(before)
        quantise(third[-1])
        make_y(1, 1)
        for g in range(GROUPS):
            make_y(last, g)
        for i in range(len(PIECES)):
            for g in range(GROUPS):
                make_planes(i, g)

        for q in range(QUADS):
            nc.scalar.dma_start(
                out_2[:, LIVE * q : LIVE * (q + 1), :].bitcast(I32).rearrange("g r n -> r g n"),
                y_sc[live(q), :, :].bitcast(I32),
            )
